import numpy as np
import ml_dtypes


def mxq(x, axis, fmt="e4m3"):
    dtype, down = {"e4m3": (ml_dtypes.float8_e4m3fn, 7), "e5m2": (ml_dtypes.float8_e5m2, 14)}[fmt]
    v = np.moveaxis(np.asarray(x, np.float32).astype(ml_dtypes.bfloat16).astype(np.float64), axis, -1)
    blocks = v.reshape(v.shape[:-1] + (-1, 32))
    amax = np.abs(blocks).max(-1, keepdims=True)
    byte = np.maximum(np.where(amax > 0, np.frexp(amax)[1] - 1 + 127, 0) - down, 1)
    scale = np.exp2(byte - 127.0)
    codes = (blocks / scale).astype(np.float32).astype(dtype).astype(np.float64)
    return np.moveaxis((codes * scale).reshape(v.shape), -1, axis)


WIDE = False


def mx_kscale(k):
    if not WIDE:
        return np.ones(k)
    levels = np.array([10, -10, 5, -5, 0])
    if k % 512:
        return np.exp2(np.random.permutation(np.resize(levels, k // 32))).repeat(32)
    a = np.empty((k // 512, 16))
    for p in range(k // 512):
        a[p, :8] = np.random.permutation(np.resize(levels, 8))
        for g in range(8):
            far = levels[np.abs(levels - a[p, g]) >= 10]
            a[p, g + 8] = far[np.random.randint(len(far))]
    return np.exp2(a.ravel()).repeat(32)


def f64(x):
    return np.asarray(x).astype(np.float64)


def striped(idx):
    return np.tile(idx.reshape(-1, 16).T, (8, 1)).astype(np.uint16)


def unstriped(offs):
    return offs[:16].T.reshape(-1).astype(np.int64)


def relu2(v):
    return np.maximum(v, 0.0) ** 2


K, T, E, C, N = 1536, 1024, 16, 256, 128
TOP = 4


def by_expert(wq, xq):
    return np.concatenate([wq[e].T @ xq[:, e * C:(e + 1) * C] for e in range(E)], axis=1)


def setup_inputs():
    n = np.random.standard_normal
    s = mx_kscale(K)[:, None]
    deal = np.repeat(np.arange(E), C).reshape(TOP, T)[:, np.random.permutation(T)]
    deal = np.take_along_axis(deal, np.argsort(np.random.rand(TOP, T), axis=0), axis=0)
    for _ in range(8):
        s_, t_ = np.random.permutation(T).reshape(2, -1); r = np.random.randint(TOP, size=T // 2); x, y = deal[r, s_].copy(), deal[r, t_].copy()
        ok = ~((deal[:, s_] == y).any(0) | (deal[:, t_] == x).any(0)); deal[r[ok], s_[ok]] = y[ok]; deal[r[ok], t_[ok]] = x[ok]
    order = np.lexsort((np.random.rand(TOP * T), deal.reshape(-1)))
    slot_token = order % T; pos = np.empty(TOP * T, np.int64); pos[order] = np.arange(TOP * T); pos = pos.reshape(TOP, T)
    g = np.random.uniform(0.5, 1.5, (TOP, T)); g = g / g.sum(0)
    w_slot = np.empty(E * C)
    for r in range(TOP): w_slot[pos[r]] = g[r]
    return {
        "xT": (n((K, T)) * s).astype(np.float32),
        "w": (n((E, K, N)) / np.sqrt(K) / s[None]).astype(np.float32),
        "b": (0.3 * n((N, E))).astype(np.float32),
        "gate": np.tile(w_slot, (K, 1)).astype(np.float32),
        "offs": striped(slot_token),
        "pos1": striped(pos[0]),
        "pos2": striped(pos[1]),
        "pos3": striped(pos[2]),
        "pos4": striped(pos[3]),
    }


def reference(xT, w, b, gate, offs, pos1, pos2, pos3, pos4):
    idx = unstriped(offs)
    xq = mxq(f64(gate) * f64(xT)[:, idx], 0, "e4m3")
    y = by_expert(mxq(f64(w), 1, "e4m3"), xq)
    y = relu2(y + np.repeat(f64(b), C, axis=1))
    return y[:, unstriped(pos1)] + y[:, unstriped(pos2)] + y[:, unstriped(pos3)] + y[:, unstriped(pos4)]

@@ -1,0 +1,240 @@
+from contextlib import ExitStack
+
+import concourse.mybir as mybir
+
+K, T, E, C, N = 1536, 1024, 16, 256, 128
+TOP = 4
+SLOTS = E * C
+
+FLOPS = 2 * K * N * SLOTS
+BYTES = 4 * (K * T + E * K * N + N * E + SLOTS + N * T) + 2 * 128 * (SLOTS + TOP * T) // 16
+
+F32 = mybir.dt.float32
+BF16 = mybir.dt.bfloat16
+U32 = mybir.dt.uint32
+U16 = mybir.dt.uint16
+U8 = mybir.dt.uint8
+FP8X4 = mybir.dt.float8_e4m3fn_x4
+MULT = mybir.AluOpType.mult
+ADD = mybir.AluOpType.add
+RELU = mybir.ActivationFunctionType.Relu
+SQUARE = mybir.ActivationFunctionType.Square
+
+P = 128
+PACK = 4
+K_PASS = P * PACK
+PASSES = K // K_PASS
+STRIPE = 16
+CHUNK_EXPERTS = 4
+CHUNK = CHUNK_EXPERTS * C
+CHUNKS = E // CHUNK_EXPERTS
+WINDOW = T + 16
+RUN = 4
+FIRST_CUT = 384
+LAST_CHUNK_WIDTHS = ((1024,), (512, 512), (512, 256, 128, 128))
+HALF = T // 2
+
+
+def make_steps():
+    steps = []
+    for chunk in range(CHUNKS):
+        for g in range(PASSES):
+            widths = LAST_CHUNK_WIDTHS[g] if chunk == CHUNKS - 1 else (CHUNK,)
+            first = chunk * CHUNK
+            for width in widths:
+                steps.append((chunk, g, first, width))
+                first += width
+    return steps
+
+
+def make_groups():
+    groups = [(e * C, C) for e in range(E - 1)]
+    groups.append(((E - 1) * C, C // 2))
+    groups.append(((E - 1) * C + C // 2, C // 2))
+    return groups
+
+
+def interleave(nc, dst, src):
+    nc.scalar.copy(
+        out=dst.rearrange("p (c i) t -> p c t i", i=RUN),
+        in_=src.rearrange("p t (c i) -> p c t i", i=RUN),
+    )
+
+
+def tile_moe_pre_lin_relu2_kernel(
+    tc, xT, w, b, gate, offs, pos1, pos2, pos3, pos4, out
+):
+    nc = tc.nc
+    steps = make_steps()
+    groups = make_groups()
+    panels = [(chunk, g) for chunk in range(CHUNKS) for g in range(PASSES)]
+
+    with ExitStack() as ctx:
+        held = ctx.enter_context(tc.tile_pool(name="held", bufs=1))
+        ring = ctx.enter_context(tc.tile_pool(name="ring", bufs=3))
+        psum = ctx.enter_context(tc.psum_pool(name="psum", bufs=8))
+
+        slot_tokens = held.tile([P, SLOTS // STRIPE], U16, name="slot_tokens")
+        token_slots = [held.tile([P, T // STRIPE], U16, name="token_slots%d" % r) for r in range(TOP)]
+        gate_sb = held.tile([P, SLOTS], F32, name="gate_sb")
+        bias = held.tile([P, E], F32, name="bias")
+        y = held.tile([P, SLOTS], F32, name="y")
+        tokens = [
+            [held.tile([P, WINDOW], F32, name="tokens%d_%d" % (g, t)) for t in range(PACK)]
+            for g in range(PASSES)
+        ]
+        x_rows = xT.rearrange("(g p t) c -> g t p c", g=PASSES, t=PACK)
+
+        w_raw, w_bf, w_codes, w_scales = {}, {}, {}, {}
+        x_f32, x_bf, x_codes, x_scales = {}, {}, {}, {}
+        sums = {}
+
+        def load_tokens(g, t):
+            nc.sync.dma_start(out=tokens[g][t][:, 0:T], in_=x_rows[g, t])
+
+        def load_gate(first, last):
+            nc.sync.dma_start(out=gate_sb[:, first:last], in_=gate[0:P, first:last])
+
+        def load_w(panel):
+            chunk, g = panel
+            w_raw[panel] = ring.tile([P, CHUNK_EXPERTS, PACK * N], F32, name="w_raw")
+            rows = w[chunk * CHUNK_EXPERTS : (chunk + 1) * CHUNK_EXPERTS, g * K_PASS : (g + 1) * K_PASS, :]
+            nc.sync.dma_start(out=w_raw[panel][:], in_=rows.rearrange("e (p t) n -> p e (t n)", t=PACK))
+
+        def round_w(panel):
+            w_bf[panel] = ring.tile([P, CHUNK_EXPERTS * N, PACK], BF16, name="w_bf", align_bytes=64)
+            for e in range(CHUNK_EXPERTS):
+                interleave(
+                    nc,
+                    w_bf[panel][:, e * N : (e + 1) * N, :],
+                    w_raw[panel][:, e, :].rearrange("p (t n) -> p t n", t=PACK),
+                )
+
+        def quantize_w(panel):
+            w_codes[panel] = ring.tile([P, CHUNK_EXPERTS * N], U32, name="w_codes", align_bytes=64)
+            w_scales[panel] = ring.tile([P, CHUNK_EXPERTS * N], U8, name="w_scales", align_bytes=64)
+            nc.vector.quantize_mx(
+                out=w_codes[panel][:].bitcast(FP8X4),
+                scales=w_scales[panel][:],
+                in_=w_bf[panel][:].rearrange("p n t -> p (n t)"),
+            )
+
+        def gather_x(s):
+            chunk, g, first, width = steps[s]
+            x_f32[s] = ring.tile([P, PACK, width], F32, name="x_f32")
+            for t in range(PACK):
+                cuts = (0, FIRST_CUT, width) if (s, t) == (0, 0) else (0, width)
+                for lo, hi in zip(cuts[:-1], cuts[1:]):
+                    offsets = slot_tokens[:, (first + lo) // STRIPE : (first + hi) // STRIPE]
+                    nc.vector.tensor_tensor(
+                        x_f32[s][:, t, lo:hi],
+                        tokens[g][t][:].indirect(offsets),
+                        gate_sb[:, first + lo : first + hi],
+                        MULT,
+                    )
+
+        def round_x(s):
+            width = steps[s][3]
+            x_bf[s] = ring.tile([P, width, PACK], BF16, name="x_bf", align_bytes=64)
+            interleave(nc, x_bf[s][:], x_f32[s][:])
+
+        def quantize_x(s):
+            width = steps[s][3]
+            x_codes[s] = ring.tile([P, width], U32, name="x_codes", align_bytes=64)
+            x_scales[s] = ring.tile([P, width], U8, name="x_scales", align_bytes=64)
+            nc.vector.quantize_mx(
+                out=x_codes[s][:].bitcast(FP8X4),
+                scales=x_scales[s][:],
+                in_=x_bf[s][:].rearrange("p c t -> p (c t)"),
+            )
+
+        def groups_of(s):
+            chunk, g, first, width = steps[s]
+            return [grp for grp in groups if first <= grp[0] < first + width]
+
+        def multiply(s):
+            chunk, g, first, width = steps[s]
+            for grp in groups_of(s):
+                start, n = grp
+                if g == 0:
+                    sums[grp] = psum.tile([P, n], F32, name="sums")
+                e = start // C - chunk * CHUNK_EXPERTS
+                w_cols = slice(e * N, (e + 1) * N)
+                x_cols = slice(start - first, start - first + n)
+                nc.tensor.matmul_mx(
+                    out=sums[grp][:],
+                    lhsT=w_codes[chunk, g][:, w_cols].bitcast(FP8X4),
+                    lhsT_scale=w_scales[chunk, g][:, w_cols],
+                    rhs=x_codes[s][:, x_cols].bitcast(FP8X4),
+                    rhs_scale=x_scales[s][:, x_cols],
+                    start=(g == 0),
+                    stop=(g == PASSES - 1),
+                )
+
+        def activate(s):
+            if steps[s][1] == PASSES - 1:
+                for grp in groups_of(s):
+                    start, n = grp
+                    e = start // C
+                    relu = ring.tile([P, n], F32, name="relu")
+                    nc.scalar.activation(relu[:], sums[grp][:], RELU, bias=bias[:, e : e + 1])
+                    nc.scalar.activation(y[:, start : start + n], relu[:], SQUARE)
+
+        nc.sync.dma_start(slot_tokens[:], offs)
+        load_gate(0, FIRST_CUT)
+        load_tokens(0, 0)
+        load_gate(FIRST_CUT, CHUNK)
+        for t in range(1, PACK):
+            load_tokens(0, t)
+        load_w(panels[0])
+        for g in range(1, PASSES):
+            for t in range(PACK):
+                load_tokens(g, t)
+            load_w(panels[g])
+        load_gate(CHUNK, SLOTS)
+        nc.sync.dma_start(out=bias[:], in_=b)
+        for r, pos in enumerate((pos1, pos2, pos3, pos4)):
+            nc.sync.dma_start(token_slots[r][:], pos)
+        for g in range(PASSES):
+            for t in range(PACK):
+                nc.vector.memset(tokens[g][t][:, T:WINDOW], 0.0)
+
+        round_w(panels[0])
+        for s in range(len(steps) + 2):
+            if s < len(steps):
+                gather_x(s)
+            if 1 <= s <= len(steps):
+                round_x(s - 1)
+                quantize_x(s - 1)
+            if s < len(panels):
+                quantize_w(panels[s])
+            if 1 <= s <= len(steps):
+                multiply(s - 1)
+            if s >= 2:
+                activate(s - 2)
+            if s + 1 < len(panels):
+                round_w(panels[s + 1])
+            if s + PASSES < len(panels):
+                load_w(panels[s + PASSES])
+
+        picked = ring.tile([P, TOP, T], F32, name="x_f32")
+        total = held.tile([P, TOP - 1, T], F32, name="total")
+
+        def pick(h, r):
+            cols = slice(h * HALF, (h + 1) * HALF)
+            offsets = token_slots[r][:, h * HALF // STRIPE : (h + 1) * HALF // STRIPE]
+            nc.vector.tensor_copy(picked[:, r, cols], y[:].indirect(offsets))
+
+        def add(h, r):
+            cols = slice(h * HALF, (h + 1) * HALF)
+            so_far = picked[:, 0, cols] if r == 1 else total[:, r - 2, cols]
+            nc.vector.tensor_tensor(total[:, r - 1, cols], so_far, picked[:, r, cols], ADD)
+            if r == TOP - 1:
+                nc.sync.dma_start(out=out[:, cols], in_=total[:, r - 1, cols])
+
+        picks = [(h, r) for h in range(2) for r in range(TOP)]
+        for i in range(len(picks) + 1):
+            if i < len(picks):
+                pick(*picks[i])
+            if i >= 1 and picks[i - 1][1] >= 1:
+                add(*picks[i - 1])

@@ -30,7 +30,7 @@ CHUNK = CHUNK_EXPERTS * C
 CHUNKS = E // CHUNK_EXPERTS
 WINDOW = T + 16
 RUN = 4
-FIRST_CUT = 384
+FIRST_CUTS = (0, 192, 512, CHUNK)
 LAST_CHUNK_WIDTHS = ((1024,), (512, 512), (512, 256, 128, 128))
 HALF = T // 2
 
@@ -102,7 +102,7 @@ def tile_moe_pre_lin_relu2_kernel(
             nc.sync.dma_start(out=w_raw[panel][:], in_=rows.rearrange("e (p t) n -> p e (t n)", t=PACK))
 
         def round_w(panel):
-            w_bf[panel] = ring.tile([P, CHUNK_EXPERTS * N, PACK], BF16, name="w_bf", align_bytes=64)
+            w_bf[panel] = ring.tile([P, CHUNK_EXPERTS * N, PACK], BF16, name="w_bf", align_bytes=64, bufs=4)
             for e in range(CHUNK_EXPERTS):
                 interleave(
                     nc,
@@ -123,7 +123,7 @@ def tile_moe_pre_lin_relu2_kernel(
             chunk, g, first, width = steps[s]
             x_f32[s] = ring.tile([P, PACK, width], F32, name="x_f32")
             for t in range(PACK):
-                cuts = (0, FIRST_CUT, width) if (s, t) == (0, 0) else (0, width)
+                cuts = FIRST_CUTS if (s, t) == (0, 0) else (0, width)
                 for lo, hi in zip(cuts[:-1], cuts[1:]):
                     offsets = slot_tokens[:, (first + lo) // STRIPE : (first + hi) // STRIPE]
                     nc.vector.tensor_tensor(
@@ -180,10 +180,10 @@ def tile_moe_pre_lin_relu2_kernel(
                     nc.scalar.activation(relu[:], sums[grp][:], RELU, bias=bias[:, e : e + 1])
                     nc.scalar.activation(y[:, start : start + n], relu[:], SQUARE)
 
-        nc.sync.dma_start(slot_tokens[:], offs)
-        load_gate(0, FIRST_CUT)
         load_tokens(0, 0)
-        load_gate(FIRST_CUT, CHUNK)
+        nc.sync.dma_start(slot_tokens[:], offs)
+        for lo, hi in zip(FIRST_CUTS[:-1], FIRST_CUTS[1:]):
+            load_gate(lo, hi)
         for t in range(1, PACK):
             load_tokens(0, t)
         load_w(panels[0])
@@ -200,6 +200,7 @@ def tile_moe_pre_lin_relu2_kernel(
                 nc.vector.memset(tokens[g][t][:, T:WINDOW], 0.0)
 
         round_w(panels[0])
+        round_w(panels[1])
         for s in range(len(steps) + 2):
             if s < len(steps):
                 gather_x(s)
@@ -212,8 +213,8 @@ def tile_moe_pre_lin_relu2_kernel(
                 multiply(s - 1)
             if s >= 2:
                 activate(s - 2)
-            if s + 1 < len(panels):
-                round_w(panels[s + 1])
+            if s + 2 < len(panels):
+                round_w(panels[s + 2])
             if s + PASSES < len(panels):
                 load_w(panels[s + PASSES])
 
@@ -225,16 +226,23 @@ def tile_moe_pre_lin_relu2_kernel(
             offsets = token_slots[r][:, h * HALF // STRIPE : (h + 1) * HALF // STRIPE]
             nc.vector.tensor_copy(picked[:, r, cols], y[:].indirect(offsets))
 
-        def add(h, r):
-            cols = slice(h * HALF, (h + 1) * HALF)
+        def add(engine, r, cols):
             so_far = picked[:, 0, cols] if r == 1 else total[:, r - 2, cols]
-            nc.vector.tensor_tensor(total[:, r - 1, cols], so_far, picked[:, r, cols], ADD)
-            if r == TOP - 1:
-                nc.sync.dma_start(out=out[:, cols], in_=total[:, r - 1, cols])
+            engine.tensor_tensor(total[:, r - 1, cols], so_far, picked[:, r, cols], ADD)
 
-        picks = [(h, r) for h in range(2) for r in range(TOP)]
-        for i in range(len(picks) + 1):
-            if i < len(picks):
-                pick(*picks[i])
-            if i >= 1 and picks[i - 1][1] >= 1:
-                add(*picks[i - 1])
+        halves = [slice(h * HALF, (h + 1) * HALF) for h in range(2)]
+        for h in range(2):
+            for r in range(TOP - 1):
+                pick(h, r)
+                if r >= 1:
+                    add(nc.gpsimd, r, halves[h])
+        for h in range(2):
+            pick(h, TOP - 1)
+        quarter = HALF // 2
+        for queue, part in (
+            (nc.sync, halves[0]),
+            (nc.scalar, slice(HALF, HALF + quarter)),
+            (nc.sync, slice(HALF + quarter, T)),
+        ):
+            add(nc.vector, TOP - 1, part)
+            queue.dma_start(out=out[:, part], in_=total[:, TOP - 2, part])

@@ -33,6 +33,7 @@ RUN = 4
 FIRST_CUTS = (0, 192, 512, CHUNK)
 LAST_CHUNK_WIDTHS = ((1024,), (512, 512), (512, 256, 128, 128))
 HALF = T // 2
+LAST_STORE = 128
 
 
 def make_steps():
@@ -218,31 +219,18 @@ def tile_moe_pre_lin_relu2_kernel(
             if s + PASSES < len(panels):
                 load_w(panels[s + PASSES])
 
-        picked = ring.tile([P, TOP, T], F32, name="x_f32")
-        total = held.tile([P, TOP - 1, T], F32, name="total")
+        partial = ring.tile([P, TOP, T], F32, name="x_f32")
 
-        def pick(h, r):
-            cols = slice(h * HALF, (h + 1) * HALF)
-            offsets = token_slots[r][:, h * HALF // STRIPE : (h + 1) * HALF // STRIPE]
-            nc.vector.tensor_copy(picked[:, r, cols], y[:].indirect(offsets))
+        def combine(r, lo, hi):
+            offsets = token_slots[r][:, lo // STRIPE : hi // STRIPE]
+            if r == 0:
+                nc.vector.tensor_copy(partial[:, 0, lo:hi], y[:].indirect(offsets))
+            else:
+                nc.vector.tensor_tensor(partial[:, r, lo:hi], y[:].indirect(offsets), partial[:, r - 1, lo:hi], ADD)
 
-        def add(engine, r, cols):
-            so_far = picked[:, 0, cols] if r == 1 else total[:, r - 2, cols]
-            engine.tensor_tensor(total[:, r - 1, cols], so_far, picked[:, r, cols], ADD)
-
-        halves = [slice(h * HALF, (h + 1) * HALF) for h in range(2)]
-        for h in range(2):
-            for r in range(TOP - 1):
-                pick(h, r)
-                if r >= 1:
-                    add(nc.gpsimd, r, halves[h])
-        for h in range(2):
-            pick(h, TOP - 1)
-        quarter = HALF // 2
-        for queue, part in (
-            (nc.sync, halves[0]),
-            (nc.scalar, slice(HALF, HALF + quarter)),
-            (nc.sync, slice(HALF + quarter, T)),
-        ):
-            add(nc.vector, TOP - 1, part)
-            queue.dma_start(out=out[:, part], in_=total[:, TOP - 2, part])
+        for r in range(TOP - 1):
+            for h in range(2):
+                combine(r, h * HALF, (h + 1) * HALF)
+        for queue, lo, hi in ((nc.sync, 0, HALF), (nc.scalar, HALF, T - LAST_STORE), (nc.sync, T - LAST_STORE, T)):
+            combine(TOP - 1, lo, hi)
+            queue.dma_start(out=out[:, lo:hi], in_=partial[:, TOP - 1, lo:hi])

@@ -25,34 +25,43 @@ PACK = 4
 K_PASS = P * PACK
 PASSES = K // K_PASS
 STRIPE = 16
-CHUNK_EXPERTS = 4
+CHUNK_EXPERTS = 8
 CHUNK = CHUNK_EXPERTS * C
-CHUNKS = E // CHUNK_EXPERTS
-WINDOW = T + 16
+WINDOW = CHUNK + 16
+SETS = 2
 RUN = 4
-FIRST_CUTS = (0, 192, 512, CHUNK)
-LAST_CHUNK_WIDTHS = ((1024,), (512, 512), (512, 256, 128, 128))
+PIECE = 1024
+W_LOAD_EXPERTS = 1
+FIRST_CUTS = (0, 128, 448, 1024, CHUNK)
 HALF = T // 2
 LAST_STORE = 128
+LAST = (E - 1) * C
 
 
 def make_steps():
-    steps = []
-    for chunk in range(CHUNKS):
-        for g in range(PASSES):
-            widths = LAST_CHUNK_WIDTHS[g] if chunk == CHUNKS - 1 else (CHUNK,)
-            first = chunk * CHUNK
-            for width in widths:
-                steps.append((chunk, g, first, width))
-                first += width
+    steps = [(g, 0, CHUNK) for g in range(PASSES)]
+    steps.append((2, CHUNK, CHUNK))
+    steps.append((1, CHUNK, CHUNK - C))
+    steps.append((0, CHUNK, 4 * C))
+    steps.append((1, LAST, C))
+    steps.append((0, CHUNK + 4 * C, 2 * C))
+    steps.append((0, CHUNK + 6 * C, C))
+    steps.append((0, LAST, C // 2))
+    steps.append((0, LAST + C // 2, C // 2))
     return steps
 
 
-def make_groups():
-    groups = [(e * C, C) for e in range(E - 1)]
-    groups.append(((E - 1) * C, C // 2))
-    groups.append(((E - 1) * C + C // 2, C // 2))
-    return groups
+def pieces_of(first, width):
+    pieces = []
+    end = first + width
+    while first < end:
+        stop = LAST if first < LAST < end else end
+        n = PIECE
+        while n > stop - first:
+            n //= 2
+        pieces.append((first, n))
+        first = first + n
+    return pieces
 
 
 def interleave(nc, dst, src):
@@ -67,8 +76,7 @@ def tile_moe_pre_lin_relu2_kernel(
 ):
     nc = tc.nc
     steps = make_steps()
-    groups = make_groups()
-    panels = [(chunk, g) for chunk in range(CHUNKS) for g in range(PASSES)]
+    panels = [(0, g) for g in range(PASSES)] + [(1, g) for g in reversed(range(PASSES))]
 
     with ExitStack() as ctx:
         held = ctx.enter_context(tc.tile_pool(name="held", bufs=1))
@@ -77,38 +85,46 @@ def tile_moe_pre_lin_relu2_kernel(
 
         slot_tokens = held.tile([P, SLOTS // STRIPE], U16, name="slot_tokens")
         token_slots = [held.tile([P, T // STRIPE], U16, name="token_slots%d" % r) for r in range(TOP)]
-        gate_sb = held.tile([P, SLOTS], F32, name="gate_sb")
         bias = held.tile([P, E], F32, name="bias")
         y = held.tile([P, SLOTS], F32, name="y")
+        gate_late = held.tile([P, CHUNK], F32, name="gate_late")
         tokens = [
-            [held.tile([P, WINDOW], F32, name="tokens%d_%d" % (g, t)) for t in range(PACK)]
-            for g in range(PASSES)
+            [held.tile([P, WINDOW], F32, name="tokens%d_%d" % (u, t), align_bytes=64) for t in range(PACK)]
+            for u in range(SETS)
         ]
         x_rows = xT.rearrange("(g p t) c -> g t p c", g=PASSES, t=PACK)
 
         w_raw, w_bf, w_codes, w_scales = {}, {}, {}, {}
         x_f32, x_bf, x_codes, x_scales = {}, {}, {}, {}
-        sums = {}
+        sums, passes_done = {}, {}
 
         def load_tokens(g, t):
-            nc.sync.dma_start(out=tokens[g][t][:, 0:T], in_=x_rows[g, t])
+            nc.sync.dma_start(out=tokens[g % SETS][t][:, 0:T], in_=x_rows[g, t])
+
+        def gate_sb(first, last):
+            if first < CHUNK:
+                return y[:, CHUNK + first : CHUNK + last]
+            return gate_late[:, first - CHUNK : last - CHUNK]
 
         def load_gate(first, last):
-            nc.sync.dma_start(out=gate_sb[:, first:last], in_=gate[0:P, first:last])
+            nc.sync.dma_start(out=gate_sb(first, last), in_=gate[0:P, first:last])
 
         def load_w(panel):
             chunk, g = panel
-            w_raw[panel] = ring.tile([P, CHUNK_EXPERTS, PACK * N], F32, name="w_raw")
-            rows = w[chunk * CHUNK_EXPERTS : (chunk + 1) * CHUNK_EXPERTS, g * K_PASS : (g + 1) * K_PASS, :]
-            nc.sync.dma_start(out=w_raw[panel][:], in_=rows.rearrange("e (p t) n -> p e (t n)", t=PACK))
+            for e0 in range(0, CHUNK_EXPERTS, W_LOAD_EXPERTS):
+                w_raw[panel, e0] = ring.tile([P, W_LOAD_EXPERTS, PACK * N], F32, name="w_raw", bufs=5)
+                first = chunk * CHUNK_EXPERTS + e0
+                rows = w[first : first + W_LOAD_EXPERTS, g * K_PASS : (g + 1) * K_PASS, :]
+                nc.sync.dma_start(out=w_raw[panel, e0][:], in_=rows.rearrange("e (p t) n -> p e (t n)", t=PACK))
 
         def round_w(panel):
-            w_bf[panel] = ring.tile([P, CHUNK_EXPERTS * N, PACK], BF16, name="w_bf", align_bytes=64, bufs=4)
+            w_bf[panel] = ring.tile([P, CHUNK_EXPERTS * N, PACK], BF16, name="w_bf", align_bytes=64, bufs=2)
             for e in range(CHUNK_EXPERTS):
+                raw = w_raw[panel, e - e % W_LOAD_EXPERTS]
                 interleave(
                     nc,
                     w_bf[panel][:, e * N : (e + 1) * N, :],
-                    w_raw[panel][:, e, :].rearrange("p (t n) -> p t n", t=PACK),
+                    raw[:, e % W_LOAD_EXPERTS, :].rearrange("p (t n) -> p t n", t=PACK),
                 )
 
         def quantize_w(panel):
@@ -121,65 +137,75 @@ def tile_moe_pre_lin_relu2_kernel(
             )
 
         def gather_x(s):
-            chunk, g, first, width = steps[s]
-            x_f32[s] = ring.tile([P, PACK, width], F32, name="x_f32")
+            g, first, width = steps[s]
+            x_f32[s] = held.tile([P, PACK, width], F32, name="x_f32_%d" % (s % 2))
             for t in range(PACK):
                 cuts = FIRST_CUTS if (s, t) == (0, 0) else (0, width)
                 for lo, hi in zip(cuts[:-1], cuts[1:]):
                     offsets = slot_tokens[:, (first + lo) // STRIPE : (first + hi) // STRIPE]
                     nc.vector.tensor_tensor(
                         x_f32[s][:, t, lo:hi],
-                        tokens[g][t][:].indirect(offsets),
-                        gate_sb[:, first + lo : first + hi],
+                        tokens[g % SETS][t][:].indirect(offsets),
+                        gate_sb(first + lo, first + hi),
                         MULT,
                     )
 
-        def round_x(s):
-            width = steps[s][3]
-            x_bf[s] = ring.tile([P, width, PACK], BF16, name="x_bf", align_bytes=64)
-            interleave(nc, x_bf[s][:], x_f32[s][:])
+        def is_late(g, start):
+            return start == LAST and g != 0
 
-        def quantize_x(s):
-            width = steps[s][3]
-            x_codes[s] = ring.tile([P, width], U32, name="x_codes", align_bytes=64)
-            x_scales[s] = ring.tile([P, width], U8, name="x_scales", align_bytes=64)
+        def round_x(s):
+            g, first, width = steps[s]
+            for start, n in pieces_of(first, width):
+                tag = "x_bf_late%d" % g if is_late(g, start) else "x_bf%d" % max(n, 2 * C)
+                pool, bufs = (held, 1) if is_late(g, start) else (ring, 2)
+                x_bf[g, start] = pool.tile([P, n, PACK], BF16, name=tag, align_bytes=64, bufs=bufs)
+                interleave(nc, x_bf[g, start][:], x_f32[s][:, :, start - first : start - first + n])
+
+        def quantize_piece(g, start, n, codes):
+            x_codes[g, start] = codes
+            x_scales[g, start] = ring.tile([P, n], U8, name="x_scales", align_bytes=64)
             nc.vector.quantize_mx(
-                out=x_codes[s][:].bitcast(FP8X4),
-                scales=x_scales[s][:],
-                in_=x_bf[s][:].rearrange("p c t -> p (c t)"),
+                out=codes.bitcast(FP8X4),
+                scales=x_scales[g, start][:],
+                in_=x_bf[g, start][:].rearrange("p c t -> p (c t)"),
             )
 
-        def groups_of(s):
-            chunk, g, first, width = steps[s]
-            return [grp for grp in groups if first <= grp[0] < first + width]
-
-        def multiply(s):
-            chunk, g, first, width = steps[s]
-            for grp in groups_of(s):
-                start, n = grp
-                if g == 0:
-                    sums[grp] = psum.tile([P, n], F32, name="sums")
-                e = start // C - chunk * CHUNK_EXPERTS
+        def multiply_piece(g, start, n):
+            size = C // 2 if start >= LAST else C
+            for lo in range(start, start + n, size):
+                done = passes_done.get(lo, 0)
+                if done == 0:
+                    sums[lo] = psum.tile([P, size], F32, name="sums")
+                chunk, e = divmod(lo // C, CHUNK_EXPERTS)
                 w_cols = slice(e * N, (e + 1) * N)
-                x_cols = slice(start - first, start - first + n)
+                x_cols = slice(lo - start, lo - start + size)
                 nc.tensor.matmul_mx(
-                    out=sums[grp][:],
+                    out=sums[lo][:],
                     lhsT=w_codes[chunk, g][:, w_cols].bitcast(FP8X4),
                     lhsT_scale=w_scales[chunk, g][:, w_cols],
-                    rhs=x_codes[s][:, x_cols].bitcast(FP8X4),
-                    rhs_scale=x_scales[s][:, x_cols],
-                    start=(g == 0),
-                    stop=(g == PASSES - 1),
+                    rhs=x_codes[g, start][:, x_cols].bitcast(FP8X4),
+                    rhs_scale=x_scales[g, start][:, x_cols],
+                    start=(done == 0),
+                    stop=(done == PASSES - 1),
                 )
+                passes_done[lo] = done + 1
 
-        def activate(s):
-            if steps[s][1] == PASSES - 1:
-                for grp in groups_of(s):
-                    start, n = grp
-                    e = start // C
-                    relu = ring.tile([P, n], F32, name="relu")
-                    nc.scalar.activation(relu[:], sums[grp][:], RELU, bias=bias[:, e : e + 1])
-                    nc.scalar.activation(y[:, start : start + n], relu[:], SQUARE)
+        def quantize_and_multiply(s):
+            g, first, width = steps[s]
+            for start, n in pieces_of(first, width):
+                if not is_late(g, start):
+                    codes = ring.tile([P, n], U32, name="x_codes", align_bytes=64)
+                    quantize_piece(g, start, n, codes[:])
+                    multiply_piece(g, start, n)
+
+        def activate_finished():
+            for lo in sorted(sums):
+                if passes_done[lo] == PASSES:
+                    size = C // 2 if lo >= LAST else C
+                    e = lo // C
+                    cols = slice(lo, lo + size)
+                    nc.scalar.activation(y[:, cols], sums.pop(lo)[:], RELU, bias=bias[:, e : e + 1])
+                    nc.scalar.activation(y[:, cols], y[:, cols], SQUARE)
 
         load_tokens(0, 0)
         nc.sync.dma_start(slot_tokens[:], offs)
@@ -188,38 +214,46 @@ def tile_moe_pre_lin_relu2_kernel(
         for t in range(1, PACK):
             load_tokens(0, t)
         load_w(panels[0])
-        for g in range(1, PASSES):
-            for t in range(PACK):
-                load_tokens(g, t)
-            load_w(panels[g])
-        load_gate(CHUNK, SLOTS)
-        nc.sync.dma_start(out=bias[:], in_=b)
-        for r, pos in enumerate((pos1, pos2, pos3, pos4)):
-            nc.sync.dma_start(token_slots[r][:], pos)
-        for g in range(PASSES):
-            for t in range(PACK):
-                nc.vector.memset(tokens[g][t][:, T:WINDOW], 0.0)
+        load_w(panels[1])
+        for t in range(PACK):
+            load_tokens(1, t)
+        for plane in tokens[0] + tokens[1]:
+            nc.gpsimd.memset(plane[:, T:WINDOW], 0.0)
 
         round_w(panels[0])
-        round_w(panels[1])
-        for s in range(len(steps) + 2):
-            if s < len(steps):
-                gather_x(s)
-            if 1 <= s <= len(steps):
+        last = len(steps) - 1
+        for s in range(last + 1):
+            gather_x(s)
+            if s + 2 < len(panels):
+                load_w(panels[s + 2])
+            if s in (0, PASSES):
+                for t in range(PACK):
+                    load_tokens(steps[s + 2][0], t)
+            if s == 1:
+                load_gate(CHUNK, SLOTS)
+                nc.sync.dma_start(out=bias[:], in_=b)
+                for r, pos in enumerate((pos1, pos2, pos3, pos4)):
+                    nc.sync.dma_start(token_slots[r][:], pos)
+            if s >= 1:
                 round_x(s - 1)
-                quantize_x(s - 1)
+                activate_finished()
+            if s + 1 < len(panels):
+                round_w(panels[s + 1])
+            if 1 <= s < last:
+                quantize_and_multiply(s - 1)
             if s < len(panels):
                 quantize_w(panels[s])
-            if 1 <= s <= len(steps):
-                multiply(s - 1)
-            if s >= 2:
-                activate(s - 2)
-            if s + 2 < len(panels):
-                round_w(panels[s + 2])
-            if s + PASSES < len(panels):
-                load_w(panels[s + PASSES])
 
-        partial = ring.tile([P, TOP, T], F32, name="x_f32")
+        round_x(last)
+        late_codes = held.tile([P, PASSES - 1, C], U32, name="tokens0_2", align_bytes=64)
+        for g in range(1, PASSES):
+            quantize_piece(g, LAST, C, late_codes[:, g - 1, :])
+            multiply_piece(g, LAST, C)
+        for s in (last - 1, last):
+            quantize_and_multiply(s)
+            activate_finished()
+
+        partial = held.tile([P, TOP, T], F32, name="x_f32_%d" % ((last + 1) % 2))
 
         def combine(r, lo, hi):
             offsets = token_slots[r][:, lo // STRIPE : hi // STRIPE]

@@ -31,11 +31,13 @@ WINDOW = CHUNK + 16
 SETS = 2
 RUN = 4
 PIECE = 1024
-W_LOAD_EXPERTS = 1
+NARROW = PIECE // 2
+RAW_BUFS = 5
 FIRST_CUTS = (0, 128, 448, 1024, CHUNK)
 HALF = T // 2
 LAST_STORE = 128
 LAST = (E - 1) * C
+LATE_LOADS_STEP = 1
 
 
 def make_steps():
@@ -64,6 +66,14 @@ def pieces_of(first, width):
     return pieces
 
 
+def group_size(first):
+    return C // 2 if first >= LAST else C
+
+
+def is_late(g, start):
+    return start == LAST and g != 0
+
+
 def interleave(nc, dst, src):
     nc.scalar.copy(
         out=dst.rearrange("p (c i) t -> p c t i", i=RUN),
@@ -76,12 +86,13 @@ def tile_moe_pre_lin_relu2_kernel(
 ):
     nc = tc.nc
     steps = make_steps()
+    last = len(steps) - 1
     panels = [(0, g) for g in range(PASSES)] + [(1, g) for g in reversed(range(PASSES))]
 
     with ExitStack() as ctx:
         held = ctx.enter_context(tc.tile_pool(name="held", bufs=1))
         ring = ctx.enter_context(tc.tile_pool(name="ring", bufs=3))
-        psum = ctx.enter_context(tc.psum_pool(name="psum", bufs=8))
+        psum = ctx.enter_context(tc.psum_pool(name="psum", bufs=CHUNK_EXPERTS))
 
         slot_tokens = held.tile([P, SLOTS // STRIPE], U16, name="slot_tokens")
         token_slots = [held.tile([P, T // STRIPE], U16, name="token_slots%d" % r) for r in range(TOP)]
@@ -101,30 +112,28 @@ def tile_moe_pre_lin_relu2_kernel(
         def load_tokens(g, t):
             nc.sync.dma_start(out=tokens[g % SETS][t][:, 0:T], in_=x_rows[g, t])
 
-        def gate_sb(first, last):
+        def gate_sb(first, stop):
             if first < CHUNK:
-                return y[:, CHUNK + first : CHUNK + last]
-            return gate_late[:, first - CHUNK : last - CHUNK]
+                return y[:, CHUNK + first : CHUNK + stop]
+            return gate_late[:, first - CHUNK : stop - CHUNK]
 
-        def load_gate(first, last):
-            nc.sync.dma_start(out=gate_sb(first, last), in_=gate[0:P, first:last])
+        def load_gate(first, stop):
+            nc.sync.dma_start(out=gate_sb(first, stop), in_=gate[0:P, first:stop])
 
         def load_w(panel):
             chunk, g = panel
-            for e0 in range(0, CHUNK_EXPERTS, W_LOAD_EXPERTS):
-                w_raw[panel, e0] = ring.tile([P, W_LOAD_EXPERTS, PACK * N], F32, name="w_raw", bufs=5)
-                first = chunk * CHUNK_EXPERTS + e0
-                rows = w[first : first + W_LOAD_EXPERTS, g * K_PASS : (g + 1) * K_PASS, :]
-                nc.sync.dma_start(out=w_raw[panel, e0][:], in_=rows.rearrange("e (p t) n -> p e (t n)", t=PACK))
+            for e in range(CHUNK_EXPERTS):
+                w_raw[panel, e] = ring.tile([P, PACK * N], F32, name="w_raw", bufs=RAW_BUFS)
+                rows = w[chunk * CHUNK_EXPERTS + e, g * K_PASS : (g + 1) * K_PASS, :]
+                nc.sync.dma_start(out=w_raw[panel, e][:], in_=rows.rearrange("(p t) n -> p (t n)", t=PACK))
 
         def round_w(panel):
             w_bf[panel] = ring.tile([P, CHUNK_EXPERTS * N, PACK], BF16, name="w_bf", align_bytes=64, bufs=2)
             for e in range(CHUNK_EXPERTS):
-                raw = w_raw[panel, e - e % W_LOAD_EXPERTS]
                 interleave(
                     nc,
                     w_bf[panel][:, e * N : (e + 1) * N, :],
-                    raw[:, e % W_LOAD_EXPERTS, :].rearrange("p (t n) -> p t n", t=PACK),
+                    w_raw[panel, e][:].rearrange("p (t n) -> p t n", t=PACK),
                 )
 
         def quantize_w(panel):
@@ -150,13 +159,10 @@ def tile_moe_pre_lin_relu2_kernel(
                         MULT,
                     )
 
-        def is_late(g, start):
-            return start == LAST and g != 0
-
         def round_x(s):
             g, first, width = steps[s]
             for start, n in pieces_of(first, width):
-                tag = "x_bf_late%d" % g if is_late(g, start) else "x_bf%d" % max(n, 2 * C)
+                tag = "x_bf_late%d" % g if is_late(g, start) else "x_bf%d" % max(n, NARROW)
                 pool, bufs = (held, 1) if is_late(g, start) else (ring, 2)
                 x_bf[g, start] = pool.tile([P, n, PACK], BF16, name=tag, align_bytes=64, bufs=bufs)
                 interleave(nc, x_bf[g, start][:], x_f32[s][:, :, start - first : start - first + n])
@@ -171,7 +177,7 @@ def tile_moe_pre_lin_relu2_kernel(
             )
 
         def multiply_piece(g, start, n):
-            size = C // 2 if start >= LAST else C
+            size = group_size(start)
             for lo in range(start, start + n, size):
                 done = passes_done.get(lo, 0)
                 if done == 0:
@@ -201,10 +207,9 @@ def tile_moe_pre_lin_relu2_kernel(
         def activate_finished():
             for lo in sorted(sums):
                 if passes_done[lo] == PASSES:
-                    size = C // 2 if lo >= LAST else C
-                    e = lo // C
-                    cols = slice(lo, lo + size)
-                    nc.scalar.activation(y[:, cols], sums.pop(lo)[:], RELU, bias=bias[:, e : e + 1])
+                    expert = lo // C
+                    cols = slice(lo, lo + group_size(lo))
+                    nc.scalar.activation(y[:, cols], sums.pop(lo)[:], RELU, bias=bias[:, expert : expert + 1])
                     nc.scalar.activation(y[:, cols], y[:, cols], SQUARE)
 
         load_tokens(0, 0)
@@ -221,7 +226,6 @@ def tile_moe_pre_lin_relu2_kernel(
             nc.gpsimd.memset(plane[:, T:WINDOW], 0.0)
 
         round_w(panels[0])
-        last = len(steps) - 1
         for s in range(last + 1):
             gather_x(s)
             if s + 2 < len(panels):
@@ -229,7 +233,7 @@ def tile_moe_pre_lin_relu2_kernel(
             if s in (0, PASSES):
                 for t in range(PACK):
                     load_tokens(steps[s + 2][0], t)
-            if s == 1:
+            if s == LATE_LOADS_STEP:
                 load_gate(CHUNK, SLOTS)
                 nc.sync.dma_start(out=bias[:], in_=b)
                 for r, pos in enumerate((pos1, pos2, pos3, pos4)):

@@ -222,8 +222,6 @@ def tile_moe_pre_lin_relu2_kernel(
         load_w(panels[1])
         for t in range(PACK):
             load_tokens(1, t)
-        for plane in tokens[0] + tokens[1]:
-            nc.gpsimd.memset(plane[:, T:WINDOW], 0.0)
 
         round_w(panels[0])
         for s in range(last + 1):

@@ -45,9 +45,8 @@ def make_steps():
     steps.append((2, CHUNK, CHUNK))
     steps.append((1, CHUNK, CHUNK - C))
     steps.append((0, CHUNK, 4 * C))
+    steps.extend((0, CHUNK + e * C, C) for e in range(4, CHUNK_EXPERTS - 1))
     steps.append((1, LAST, C))
-    steps.append((0, CHUNK + 4 * C, 2 * C))
-    steps.append((0, CHUNK + 6 * C, C))
     steps.append((0, LAST, C // 2))
     steps.append((0, LAST + C // 2, C // 2))
     return steps

@@ -25,52 +25,46 @@ PACK = 4
 K_PASS = P * PACK
 PASSES = K // K_PASS
 STRIPE = 16
-CHUNK_EXPERTS = 8
-CHUNK = CHUNK_EXPERTS * C
-WINDOW = CHUNK + 16
-SETS = 2
-RUN = 4
+HALF_E = E // 2
+CHUNK = HALF_E * C
 PIECE = 1024
-NARROW = PIECE // 2
-RAW_BUFS = 5
+BANK = 512
+SPARE = 16
+RUN = 4
+DETOUR = HALF_E - 3
 FIRST_CUTS = (0, 128, 448, 1024, CHUNK)
+CLOSING_WIDTHS = (1024, 1024, 512, 512, 512, 256, 128, 128)
 HALF = T // 2
 LAST_STORE = 128
 LAST = (E - 1) * C
-LATE_LOADS_STEP = 1
 
 
 def make_steps():
-    steps = [(g, 0, CHUNK) for g in range(PASSES)]
-    steps.append((2, CHUNK, CHUNK))
-    steps.append((1, CHUNK, CHUNK - C))
-    steps.append((0, CHUNK, 4 * C))
-    steps.extend((0, CHUNK + e * C, C) for e in range(4, CHUNK_EXPERTS - 1))
-    steps.append((1, LAST, C))
-    steps.append((0, LAST, C // 2))
-    steps.append((0, LAST + C // 2, C // 2))
+    steps = [(g, first, CHUNK) for g in range(PASSES - 1) for first in (0, CHUNK)]
+    first = 0
+    for width in CLOSING_WIDTHS:
+        steps.append((PASSES - 1, first, width))
+        first = first + width
     return steps
 
 
-def pieces_of(first, width):
-    pieces = []
-    end = first + width
-    while first < end:
-        stop = LAST if first < LAST < end else end
+def powers_of_two(first, stop):
+    runs = []
+    while first < stop:
         n = PIECE
         while n > stop - first:
             n //= 2
-        pieces.append((first, n))
+        runs.append((first, n))
         first = first + n
-    return pieces
+    return runs
 
 
-def group_size(first):
-    return C // 2 if first >= LAST else C
-
-
-def is_late(g, start):
-    return start == LAST and g != 0
+def sum_of(slot):
+    if slot >= LAST:
+        return slot - slot % (C // 2), C // 2
+    if slot >= LAST - C:
+        return LAST - C, C
+    return slot - slot % BANK, BANK
 
 
 def interleave(nc, dst, src):
@@ -86,30 +80,32 @@ def tile_moe_pre_lin_relu2_kernel(
     nc = tc.nc
     steps = make_steps()
     last = len(steps) - 1
-    panels = [(0, g) for g in range(PASSES)] + [(1, g) for g in reversed(range(PASSES))]
+    panels = [(chunk, g) for g in range(PASSES) for chunk in range(2)]
 
     with ExitStack() as ctx:
         held = ctx.enter_context(tc.tile_pool(name="held", bufs=1))
-        ring = ctx.enter_context(tc.tile_pool(name="ring", bufs=3))
-        psum = ctx.enter_context(tc.psum_pool(name="psum", bufs=CHUNK_EXPERTS))
+        psum = ctx.enter_context(tc.psum_pool(name="psum", bufs=8))
 
         slot_tokens = held.tile([P, SLOTS // STRIPE], U16, name="slot_tokens")
         token_slots = [held.tile([P, T // STRIPE], U16, name="token_slots%d" % r) for r in range(TOP)]
         bias = held.tile([P, E], F32, name="bias")
         y = held.tile([P, SLOTS], F32, name="y")
         gate_late = held.tile([P, CHUNK], F32, name="gate_late")
+        windows = [CHUNK + SPARE] * (PASSES - 1) + [max(CLOSING_WIDTHS) + SPARE]
         tokens = [
-            [held.tile([P, WINDOW], F32, name="tokens%d_%d" % (u, t), align_bytes=64) for t in range(PACK)]
-            for u in range(SETS)
+            [held.tile([P, windows[g]], F32, name="tokens%d_%d" % (g, t), align_bytes=64) for t in range(PACK)]
+            for g in range(PASSES)
         ]
         x_rows = xT.rearrange("(g p t) c -> g t p c", g=PASSES, t=PACK)
 
         w_raw, w_bf, w_codes, w_scales = {}, {}, {}, {}
-        x_f32, x_bf, x_codes, x_scales = {}, {}, {}, {}
-        sums, passes_done = {}, {}
+        x_f32, x_bf, late_bf = {}, {}, {}
+        sums, done = {}, {}
+        coded = []
+        late_tags = {1: "late", 3: "tokens0_0"}
 
         def load_tokens(g, t):
-            nc.sync.dma_start(out=tokens[g % SETS][t][:, 0:T], in_=x_rows[g, t])
+            nc.sync.dma_start(out=tokens[g][t][:, 0:T], in_=x_rows[g, t])
 
         def gate_sb(first, stop):
             if first < CHUNK:
@@ -119,97 +115,114 @@ def tile_moe_pre_lin_relu2_kernel(
         def load_gate(first, stop):
             nc.sync.dma_start(out=gate_sb(first, stop), in_=gate[0:P, first:stop])
 
-        def load_w(panel):
-            chunk, g = panel
-            for e in range(CHUNK_EXPERTS):
-                w_raw[panel, e] = ring.tile([P, PACK * N], F32, name="w_raw", bufs=RAW_BUFS)
-                rows = w[chunk * CHUNK_EXPERTS + e, g * K_PASS : (g + 1) * K_PASS, :]
-                nc.sync.dma_start(out=w_raw[panel, e][:], in_=rows.rearrange("(p t) n -> p (t n)", t=PACK))
+        def load_w(i, experts, dst):
+            chunk, g = panels[i]
+            for j, e in enumerate(experts):
+                rows = w[chunk * HALF_E + e, g * K_PASS : (g + 1) * K_PASS, :]
+                nc.sync.dma_start(out=dst[:, j, :], in_=rows.rearrange("(p t) n -> p (t n)", t=PACK))
+                w_raw[i, e] = dst[:, j, :]
 
-        def round_w(panel):
-            w_bf[panel] = ring.tile([P, CHUNK_EXPERTS * N, PACK], BF16, name="w_bf", align_bytes=64, bufs=2)
-            for e in range(CHUNK_EXPERTS):
-                interleave(
-                    nc,
-                    w_bf[panel][:, e * N : (e + 1) * N, :],
-                    w_raw[panel, e][:].rearrange("p (t n) -> p t n", t=PACK),
-                )
+        def load_next_panel(s, free_gather_buffer):
+            load_w(s + 1, [DETOUR], free_gather_buffer)
+            others = [e for e in range(HALF_E) if e != DETOUR]
+            if s in late_tags:
+                aside = held.tile([P, 1, PACK * N], F32, name=late_tags[s], align_bytes=64)
+                load_w(s + 1, [DETOUR + 1], aside)
+                others.remove(DETOUR + 1)
+            staged = held.tile([P, len(others), PACK * N], F32, name="x_bf%d" % (s % 2), align_bytes=64)
+            load_w(s + 1, others, staged)
 
-        def quantize_w(panel):
-            w_codes[panel] = ring.tile([P, CHUNK_EXPERTS * N], U32, name="w_codes", align_bytes=64)
-            w_scales[panel] = ring.tile([P, CHUNK_EXPERTS * N], U8, name="w_scales", align_bytes=64)
+        def round_w(i):
+            w_bf[i] = held.tile([P, HALF_E * N, PACK], BF16, name="x_bf1" if i == 0 else "w_bf", align_bytes=64)
+            for e in range(HALF_E):
+                interleave(nc, w_bf[i][:, e * N : (e + 1) * N, :], w_raw[i, e].rearrange("p (t n) -> p t n", t=PACK))
+
+        def quantize_w(i):
+            tag = ("w_codes0", "w_codes1", "w_codes2", "tokens0_1", "w_codes0", "w_codes2")[i]
+            w_codes[panels[i]] = held.tile([P, HALF_E * N], U32, name=tag, align_bytes=64)
+            w_scales[panels[i]] = held.tile([P, HALF_E * N], U8, name="w_scales%d" % (0, 1, 2, 3, 0, 2)[i], align_bytes=64)
             nc.vector.quantize_mx(
-                out=w_codes[panel][:].bitcast(FP8X4),
-                scales=w_scales[panel][:],
-                in_=w_bf[panel][:].rearrange("p n t -> p (n t)"),
+                out=w_codes[panels[i]][:].bitcast(FP8X4),
+                scales=w_scales[panels[i]][:],
+                in_=w_bf[i][:].rearrange("p n t -> p (n t)"),
             )
 
         def gather_x(s):
             g, first, width = steps[s]
-            x_f32[s] = held.tile([P, PACK, width], F32, name="x_f32_%d" % (s % 2))
+            x_f32[s] = held.tile([P, PACK, width], F32, name="x_f32_%d" % (s % 2), align_bytes=64)
             for t in range(PACK):
                 cuts = FIRST_CUTS if (s, t) == (0, 0) else (0, width)
                 for lo, hi in zip(cuts[:-1], cuts[1:]):
                     offsets = slot_tokens[:, (first + lo) // STRIPE : (first + hi) // STRIPE]
                     nc.vector.tensor_tensor(
                         x_f32[s][:, t, lo:hi],
-                        tokens[g % SETS][t][:].indirect(offsets),
+                        tokens[g][t][:].indirect(offsets),
                         gate_sb(first + lo, first + hi),
                         MULT,
                     )
 
+        def on_time(s):
+            g, first, width = steps[s]
+            stop = first + width if g == PASSES - 1 else min(first + width, LAST)
+            return [(lo, min(PIECE, stop - lo)) for lo in range(first, stop, PIECE)]
+
         def round_x(s):
             g, first, width = steps[s]
-            for start, n in pieces_of(first, width):
-                tag = "x_bf_late%d" % g if is_late(g, start) else "x_bf%d" % max(n, NARROW)
-                pool, bufs = (held, 1) if is_late(g, start) else (ring, 2)
-                x_bf[g, start] = pool.tile([P, n, PACK], BF16, name=tag, align_bytes=64, bufs=bufs)
-                interleave(nc, x_bf[g, start][:], x_f32[s][:, :, start - first : start - first + n])
+            x_bf[s] = held.tile([P, width, PACK], BF16, name="x_bf%d" % (s % 2), align_bytes=64)
+            for lo, n in on_time(s):
+                cols = slice(lo - first, lo - first + n)
+                interleave(nc, x_bf[s][:, cols, :], x_f32[s][:, :, cols])
+            if g < PASSES - 1 and first + width > LAST:
+                late_bf[g] = held.tile([P, C, PACK], BF16, name=late_tags[s], align_bytes=64)
+                interleave(nc, late_bf[g][:], x_f32[s][:, :, LAST - first : width])
 
-        def quantize_piece(g, start, n, codes):
-            x_codes[g, start] = codes
-            x_scales[g, start] = ring.tile([P, n], U8, name="x_scales", align_bytes=64)
-            nc.vector.quantize_mx(
-                out=codes.bitcast(FP8X4),
-                scales=x_scales[g, start][:],
-                in_=x_bf[g, start][:].rearrange("p c t -> p (c t)"),
-            )
-
-        def multiply_piece(g, start, n):
-            size = group_size(start)
-            for lo in range(start, start + n, size):
-                done = passes_done.get(lo, 0)
-                if done == 0:
-                    sums[lo] = psum.tile([P, size], F32, name="sums")
-                chunk, e = divmod(lo // C, CHUNK_EXPERTS)
+        def quantize_and_multiply(g, first, n, values, codes, scales):
+            nc.vector.quantize_mx(out=codes.bitcast(FP8X4), scales=scales, in_=values.rearrange("p c t -> p (c t)"))
+            size = C // 2 if first >= LAST else C
+            for lo in range(first, first + n, size):
+                base, width = sum_of(lo)
+                if base not in done:
+                    sums[base] = psum.tile([P, width], F32, name="sums")
+                    done[base] = 0
+                chunk, e = divmod(lo // C, HALF_E)
                 w_cols = slice(e * N, (e + 1) * N)
-                x_cols = slice(lo - start, lo - start + size)
+                x_cols = slice(lo - first, lo - first + size)
                 nc.tensor.matmul_mx(
-                    out=sums[lo][:],
+                    out=sums[base][:, lo - base : lo - base + size],
                     lhsT=w_codes[chunk, g][:, w_cols].bitcast(FP8X4),
                     lhsT_scale=w_scales[chunk, g][:, w_cols],
-                    rhs=x_codes[g, start][:, x_cols].bitcast(FP8X4),
-                    rhs_scale=x_scales[g, start][:, x_cols],
-                    start=(done == 0),
-                    stop=(done == PASSES - 1),
+                    rhs=codes[:, x_cols].bitcast(FP8X4),
+                    rhs_scale=scales[:, x_cols],
+                    start=(done[base] == 0),
+                    stop=(done[base] + size == PASSES * width),
                 )
-                passes_done[lo] = done + 1
+                done[base] = done[base] + size
 
-        def quantize_and_multiply(s):
+        def multiply_step(s):
             g, first, width = steps[s]
-            for start, n in pieces_of(first, width):
-                if not is_late(g, start):
-                    codes = ring.tile([P, n], U32, name="x_codes", align_bytes=64)
-                    quantize_piece(g, start, n, codes[:])
-                    multiply_piece(g, start, n)
+            for lo, n in on_time(s):
+                codes = held.tile([P, n], U32, name="x_codes%d" % (len(coded) % 2), align_bytes=64)
+                scales = held.tile([P, n], U8, name="x_scales%d" % (len(coded) % 2), align_bytes=64)
+                coded.append(codes)
+                for start, m in powers_of_two(lo, lo + n):
+                    cols = slice(start - lo, start - lo + m)
+                    quantize_and_multiply(g, start, m, x_bf[s][:, start - first : start - first + m, :], codes[:, cols], scales[:, cols])
 
         def activate_finished():
-            for lo in sorted(sums):
-                if passes_done[lo] == PASSES:
-                    expert = lo // C
-                    cols = slice(lo, lo + group_size(lo))
-                    nc.scalar.activation(y[:, cols], sums.pop(lo)[:], RELU, bias=bias[:, expert : expert + 1])
-                    nc.scalar.activation(y[:, cols], y[:, cols], SQUARE)
+            for base in sorted(sums):
+                width = sum_of(base)[1]
+                if done[base] == PASSES * width:
+                    bank = sums.pop(base)
+                    size = min(width, C)
+                    for lo in range(0, width, size):
+                        expert = (base + lo) // C
+                        nc.scalar.activation(
+                            y[:, base + lo : base + lo + size],
+                            bank[:, lo : lo + size],
+                            RELU,
+                            bias=bias[:, expert : expert + 1],
+                        )
+                    nc.scalar.activation(y[:, base : base + width], y[:, base : base + width], SQUARE)
 
         load_tokens(0, 0)
         nc.sync.dma_start(slot_tokens[:], offs)
@@ -217,44 +230,47 @@ def tile_moe_pre_lin_relu2_kernel(
             load_gate(lo, hi)
         for t in range(1, PACK):
             load_tokens(0, t)
-        load_w(panels[0])
-        load_w(panels[1])
+        first_raw = held.tile([P, HALF_E + 1, PACK * N], F32, name="x_f32_1", align_bytes=64)
+        load_w(0, range(HALF_E), first_raw[:, 0:HALF_E, :])
+        load_next_panel(0, first_raw[:, HALF_E:, :])
+        load_gate(CHUNK, SLOTS)
         for t in range(PACK):
             load_tokens(1, t)
 
-        round_w(panels[0])
+        round_w(0)
         for s in range(last + 1):
             gather_x(s)
-            if s + 2 < len(panels):
-                load_w(panels[s + 2])
-            if s in (0, PASSES):
-                for t in range(PACK):
-                    load_tokens(steps[s + 2][0], t)
-            if s == LATE_LOADS_STEP:
-                load_gate(CHUNK, SLOTS)
-                nc.sync.dma_start(out=bias[:], in_=b)
-                for r, pos in enumerate((pos1, pos2, pos3, pos4)):
-                    nc.sync.dma_start(token_slots[r][:], pos)
             if s >= 1:
                 round_x(s - 1)
                 activate_finished()
-            if s + 1 < len(panels):
-                round_w(panels[s + 1])
+            if 1 <= s < len(panels) - 1:
+                free = held.tile([P, 1, PACK * N], F32, name="x_f32_%d" % ((s + 1) % 2), align_bytes=64)
+                load_next_panel(s, free)
+            if s == 1:
+                for t in range(PACK):
+                    load_tokens(2, t)
+                nc.sync.dma_start(out=bias[:], in_=b)
+                for r, pos in enumerate((pos1, pos2, pos3, pos4)):
+                    nc.sync.dma_start(token_slots[r][:], pos)
+            if s < len(panels) - 1:
+                round_w(s + 1)
             if 1 <= s < last:
-                quantize_and_multiply(s - 1)
-            if s < len(panels):
-                quantize_w(panels[s])
+                multiply_step(s - 1)
+            if s == 0:
+                quantize_w(0)
+            if s < len(panels) - 1:
+                quantize_w(s + 1)
 
         round_x(last)
-        late_codes = held.tile([P, PASSES - 1, C], U32, name="tokens0_2", align_bytes=64)
-        for g in range(1, PASSES):
-            quantize_piece(g, LAST, C, late_codes[:, g - 1, :])
-            multiply_piece(g, LAST, C)
+        late_codes = held.tile([P, PASSES - 1, C], U32, name="tokens2_2", align_bytes=64)
+        late_scales = held.tile([P, PASSES - 1, C], U8, name="late_scales", align_bytes=64)
+        for g in range(PASSES - 1):
+            quantize_and_multiply(g, LAST, C, late_bf[g][:], late_codes[:, g, :], late_scales[:, g, :])
         for s in (last - 1, last):
-            quantize_and_multiply(s)
+            multiply_step(s)
             activate_finished()
 
-        partial = held.tile([P, TOP, T], F32, name="x_f32_%d" % ((last + 1) % 2))
+        partial = held.tile([P, TOP, T], F32, name="x_f32_%d" % ((last + 1) % 2), align_bytes=64)
 
         def combine(r, lo, hi):
             offsets = token_slots[r][:, lo // STRIPE : hi // STRIPE]

@@ -1,6 +1,7 @@
 from contextlib import ExitStack
 
 import concourse.mybir as mybir
+from concourse.masks import make_identity
 
 K, T, E, C, N = 1536, 1024, 16, 256, 128
 TOP = 4
@@ -17,6 +18,7 @@ U8 = mybir.dt.uint8
 FP8X4 = mybir.dt.float8_e4m3fn_x4
 MULT = mybir.AluOpType.mult
 ADD = mybir.AluOpType.add
+COPY = mybir.ActivationFunctionType.Copy
 RELU = mybir.ActivationFunctionType.Relu
 SQUARE = mybir.ActivationFunctionType.Square
 
@@ -25,53 +27,36 @@ PACK = 4
 K_PASS = P * PACK
 PASSES = K // K_PASS
 STRIPE = 16
-HALF_E = E // 2
-CHUNK = HALF_E * C
-PIECE = 1024
+CHUNK_E = 4
+CHUNK = CHUNK_E * C
+CHUNKS = E // CHUNK_E
 BANK = 512
 SPARE = 16
 RUN = 4
-DETOUR = HALF_E - 3
-FIRST_CUTS = (0, 128, 448, 1024, CHUNK)
-CLOSING_WIDTHS = (1024, 1024, 512, 512, 512, 256, 128, 128)
-HALF = T // 2
-LAST_STORE = 128
+GATE_BANKS = 3
+VECTOR_SHARE = 576
+CLOSING_WIDTHS = (512, 256, 128, 128)
+TOKEN_CUTS = (0, 128, 384, 640, 896, 1024)
 LAST = (E - 1) * C
 
 
 def make_steps():
-    steps = [(g, first, CHUNK) for g in range(PASSES - 1) for first in (0, CHUNK)]
-    first = 0
+    steps = [(g, chunk * CHUNK, CHUNK) for chunk in range(CHUNKS) for g in range(PASSES)][:-1]
+    first = SLOTS - CHUNK
     for width in CLOSING_WIDTHS:
         steps.append((PASSES - 1, first, width))
         first = first + width
     return steps
 
 
-def powers_of_two(first, stop):
-    runs = []
-    while first < stop:
-        n = PIECE
-        while n > stop - first:
-            n //= 2
-        runs.append((first, n))
-        first = first + n
-    return runs
-
-
 def sum_of(slot):
+    if slot >= LAST + C // 2:
+        return LAST + C // 2, C // 2, (SLOTS // BANK) % GATE_BANKS
     if slot >= LAST:
-        return slot - slot % (C // 2), C // 2
+        return LAST, C // 2, 7
     if slot >= LAST - C:
-        return LAST - C, C
-    return slot - slot % BANK, BANK
-
-
-def interleave(nc, dst, src):
-    nc.scalar.copy(
-        out=dst.rearrange("p (c i) t -> p c t i", i=RUN),
-        in_=src.rearrange("p t (c i) -> p c t i", i=RUN),
-    )
+        return LAST - C, C, 6
+    return slot - slot % BANK, BANK, GATE_BANKS + (slot // BANK) % 4
 
 
 def tile_moe_pre_lin_relu2_kernel(
@@ -80,141 +65,140 @@ def tile_moe_pre_lin_relu2_kernel(
     nc = tc.nc
     steps = make_steps()
     last = len(steps) - 1
-    panels = [(chunk, g) for g in range(PASSES) for chunk in range(2)]
 
     with ExitStack() as ctx:
         held = ctx.enter_context(tc.tile_pool(name="held", bufs=1))
-        psum = ctx.enter_context(tc.psum_pool(name="psum", bufs=8))
+        three = ctx.enter_context(tc.tile_pool(name="three", bufs=3))
+        two = ctx.enter_context(tc.tile_pool(name="two", bufs=2))
+        psum = ctx.enter_context(tc.psum_pool(name="psum", bufs=1))
 
         slot_tokens = held.tile([P, SLOTS // STRIPE], U16, name="slot_tokens")
         token_slots = [held.tile([P, T // STRIPE], U16, name="token_slots%d" % r) for r in range(TOP)]
         bias = held.tile([P, E], F32, name="bias")
+        identity = held.tile([P, P], F32, name="identity")
+        gate_cols = held.tile([P, SLOTS // BANK, RUN], F32, name="gate_cols")
         y = held.tile([P, SLOTS], F32, name="y")
-        gate_late = held.tile([P, CHUNK], F32, name="gate_late")
-        windows = [CHUNK + SPARE] * (PASSES - 1) + [max(CLOSING_WIDTHS) + SPARE]
         tokens = [
-            [held.tile([P, windows[g]], F32, name="tokens%d_%d" % (g, t), align_bytes=64) for t in range(PACK)]
+            [held.tile([P, T + SPARE], F32, name="tokens%d_%d" % (g, t), align_bytes=64) for t in range(PACK)]
             for g in range(PASSES)
         ]
         x_rows = xT.rearrange("(g p t) c -> g t p c", g=PASSES, t=PACK)
 
         w_raw, w_bf, w_codes, w_scales = {}, {}, {}, {}
-        x_f32, x_bf, late_bf = {}, {}, {}
+        x_f32, x_bf, gate_rows = {}, {}, {}
         sums, done = {}, {}
-        coded = []
-        late_tags = {1: "late", 3: "tokens0_0"}
+
+        def panel(s):
+            g, first, width = steps[s]
+            return first // CHUNK, g
 
         def load_tokens(g, t):
             nc.sync.dma_start(out=tokens[g][t][:, 0:T], in_=x_rows[g, t])
 
-        def gate_sb(first, stop):
-            if first < CHUNK:
-                return y[:, CHUNK + first : CHUNK + stop]
-            return gate_late[:, first - CHUNK : stop - CHUNK]
+        def load_w(key):
+            chunk, g = key
+            w_raw[key] = three.tile([P, CHUNK_E, PACK * N], F32, name="w_raw", align_bytes=64)
+            rows = w[chunk * CHUNK_E : (chunk + 1) * CHUNK_E, g * K_PASS : (g + 1) * K_PASS, :]
+            nc.sync.dma_start(out=w_raw[key][:], in_=rows.rearrange("e (p t) n -> p e (t n)", t=PACK))
 
-        def load_gate(first, stop):
-            nc.sync.dma_start(out=gate_sb(first, stop), in_=gate[0:P, first:stop])
-
-        def load_w(i, experts, dst):
-            chunk, g = panels[i]
-            for j, e in enumerate(experts):
-                rows = w[chunk * HALF_E + e, g * K_PASS : (g + 1) * K_PASS, :]
-                nc.sync.dma_start(out=dst[:, j, :], in_=rows.rearrange("(p t) n -> p (t n)", t=PACK))
-                w_raw[i, e] = dst[:, j, :]
-
-        def load_next_panel(s, free_gather_buffer):
-            load_w(s + 1, [DETOUR], free_gather_buffer)
-            others = [e for e in range(HALF_E) if e != DETOUR]
-            if s in late_tags:
-                aside = held.tile([P, 1, PACK * N], F32, name=late_tags[s], align_bytes=64)
-                load_w(s + 1, [DETOUR + 1], aside)
-                others.remove(DETOUR + 1)
-            staged = held.tile([P, len(others), PACK * N], F32, name="x_bf%d" % (s % 2), align_bytes=64)
-            load_w(s + 1, others, staged)
-
-        def round_w(i):
-            w_bf[i] = held.tile([P, HALF_E * N, PACK], BF16, name="x_bf1" if i == 0 else "w_bf", align_bytes=64)
-            for e in range(HALF_E):
-                interleave(nc, w_bf[i][:, e * N : (e + 1) * N, :], w_raw[i, e].rearrange("p (t n) -> p t n", t=PACK))
-
-        def quantize_w(i):
-            tag = ("w_codes0", "w_codes1", "w_codes2", "tokens0_1", "w_codes0", "w_codes2")[i]
-            w_codes[panels[i]] = held.tile([P, HALF_E * N], U32, name=tag, align_bytes=64)
-            w_scales[panels[i]] = held.tile([P, HALF_E * N], U8, name="w_scales%d" % (0, 1, 2, 3, 0, 2)[i], align_bytes=64)
-            nc.vector.quantize_mx(
-                out=w_codes[panels[i]][:].bitcast(FP8X4),
-                scales=w_scales[panels[i]][:],
-                in_=w_bf[i][:].rearrange("p n t -> p (n t)"),
+        def round_w(key):
+            w_bf[key] = two.tile([P, CHUNK_E * N, PACK], BF16, name="w_bf", align_bytes=64)
+            nc.vector.tensor_copy(
+                out=w_bf[key][:].rearrange("p (e c i) t -> p e c t i", e=CHUNK_E, i=RUN),
+                in_=w_raw[key][:].rearrange("p e (t c i) -> p e c t i", t=PACK, i=RUN),
             )
+
+        def quantize_w(key):
+            w_codes[key] = three.tile([P, CHUNK_E * N], U32, name="w_codes", align_bytes=64)
+            w_scales[key] = three.tile([P, CHUNK_E * N], U8, name="w_scales", align_bytes=64)
+            nc.vector.quantize_mx(
+                out=w_codes[key][:].bitcast(FP8X4),
+                scales=w_scales[key][:],
+                in_=w_bf[key][:].rearrange("p n t -> p (n t)"),
+            )
+
+        def spread_gate(block):
+            gate_rows[block] = psum.tile([P, RUN, P], F32, name="bank%d" % (block % GATE_BANKS))
+            for i in range(RUN):
+                column = gate_cols[:, block, i : i + 1].to_broadcast([P, P])
+                nc.tensor.transpose(gate_rows[block][:, i, :], column, identity[:])
+
+        def gather(s, t, lo, hi, on_vector):
+            g, first, width = steps[s]
+            window = tokens[g][t][:].indirect(slot_tokens[:, (first + lo) // STRIPE : (first + hi) // STRIPE])
+            if on_vector:
+                nc.vector.tensor_copy(x_f32[s][:, t, lo:hi], window)
+            else:
+                nc.scalar.activation(x_f32[s][:, t, lo:hi], window, COPY)
 
         def gather_x(s):
             g, first, width = steps[s]
-            x_f32[s] = held.tile([P, PACK, width], F32, name="x_f32_%d" % (s % 2), align_bytes=64)
+            x_f32[s] = three.tile([P, PACK, width], F32, name="x_f32", align_bytes=64)
             for t in range(PACK):
-                cuts = FIRST_CUTS if (s, t) == (0, 0) else (0, width)
-                for lo, hi in zip(cuts[:-1], cuts[1:]):
-                    offsets = slot_tokens[:, (first + lo) // STRIPE : (first + hi) // STRIPE]
-                    nc.vector.tensor_tensor(
-                        x_f32[s][:, t, lo:hi],
-                        tokens[g][t][:].indirect(offsets),
-                        gate_sb(first + lo, first + hi),
-                        MULT,
-                    )
+                if s == 0:
+                    share = width // 2
+                elif t == 0 and width == CHUNK:
+                    share = VECTOR_SHARE
+                else:
+                    share = 0
+                gather(s, t, share, width, False)
+                if share:
+                    gather(s, t, 0, share, True)
 
-        def on_time(s):
+        def gate_and_round(s):
             g, first, width = steps[s]
-            stop = first + width if g == PASSES - 1 else min(first + width, LAST)
-            return [(lo, min(PIECE, stop - lo)) for lo in range(first, stop, PIECE)]
+            x_bf[s] = two.tile([P, width, PACK], BF16, name="x_bf", align_bytes=64)
+            for lo in range(0, width, BANK):
+                n = min(BANK, width - lo)
+                block, start = divmod(first + lo, BANK)
+                rows = gate_rows[block][:, :, start // RUN : (start + n) // RUN].rearrange("p i c -> p c i")
+                nc.vector.tensor_tensor(
+                    x_bf[s][:, lo : lo + n, :].rearrange("p (c i) t -> p c t i", i=RUN),
+                    x_f32[s][:, :, lo : lo + n].rearrange("p t (c i) -> p c t i", i=RUN),
+                    rows.unsqueeze(2).to_broadcast([P, n // RUN, PACK, RUN]),
+                    MULT,
+                )
 
-        def round_x(s):
+        def quantize_and_multiply(s):
             g, first, width = steps[s]
-            x_bf[s] = held.tile([P, width, PACK], BF16, name="x_bf%d" % (s % 2), align_bytes=64)
-            for lo, n in on_time(s):
-                cols = slice(lo - first, lo - first + n)
-                interleave(nc, x_bf[s][:, cols, :], x_f32[s][:, :, cols])
-            if g < PASSES - 1 and first + width > LAST:
-                late_bf[g] = held.tile([P, C, PACK], BF16, name=late_tags[s], align_bytes=64)
-                interleave(nc, late_bf[g][:], x_f32[s][:, :, LAST - first : width])
+            codes = two.tile([P, width], U32, name="x_codes", align_bytes=64)
+            scales = two.tile([P, width], U8, name="x_scales", align_bytes=64)
+            nc.vector.quantize_mx(
+                out=codes[:].bitcast(FP8X4), scales=scales[:], in_=x_bf[s][:].rearrange("p c t -> p (c t)")
+            )
+            return codes, scales
 
-        def quantize_and_multiply(g, first, n, values, codes, scales):
-            nc.vector.quantize_mx(out=codes.bitcast(FP8X4), scales=scales, in_=values.rearrange("p c t -> p (c t)"))
-            size = C // 2 if first >= LAST else C
-            for lo in range(first, first + n, size):
-                base, width = sum_of(lo)
+        def multiply(s, codes, scales):
+            g, first, width = steps[s]
+            lo = first
+            while lo < first + width:
+                base, group, bank = sum_of(lo)
+                size = min(group, C)
                 if base not in done:
-                    sums[base] = psum.tile([P, width], F32, name="sums")
+                    sums[base] = psum.tile([P, group], F32, name="bank%d" % bank)
                     done[base] = 0
-                chunk, e = divmod(lo // C, HALF_E)
+                e = (lo // C) % CHUNK_E
                 w_cols = slice(e * N, (e + 1) * N)
                 x_cols = slice(lo - first, lo - first + size)
                 nc.tensor.matmul_mx(
                     out=sums[base][:, lo - base : lo - base + size],
-                    lhsT=w_codes[chunk, g][:, w_cols].bitcast(FP8X4),
-                    lhsT_scale=w_scales[chunk, g][:, w_cols],
+                    lhsT=w_codes[panel(s)][:, w_cols].bitcast(FP8X4),
+                    lhsT_scale=w_scales[panel(s)][:, w_cols],
                     rhs=codes[:, x_cols].bitcast(FP8X4),
                     rhs_scale=scales[:, x_cols],
                     start=(done[base] == 0),
-                    stop=(done[base] + size == PASSES * width),
+                    stop=(done[base] + size == PASSES * group),
                 )
                 done[base] = done[base] + size
-
-        def multiply_step(s):
-            g, first, width = steps[s]
-            for lo, n in on_time(s):
-                codes = held.tile([P, n], U32, name="x_codes%d" % (len(coded) % 2), align_bytes=64)
-                scales = held.tile([P, n], U8, name="x_scales%d" % (len(coded) % 2), align_bytes=64)
-                coded.append(codes)
-                for start, m in powers_of_two(lo, lo + n):
-                    cols = slice(start - lo, start - lo + m)
-                    quantize_and_multiply(g, start, m, x_bf[s][:, start - first : start - first + m, :], codes[:, cols], scales[:, cols])
+                lo = lo + size
 
         def activate_finished():
             for base in sorted(sums):
-                width = sum_of(base)[1]
-                if done[base] == PASSES * width:
+                group = sum_of(base)[1]
+                if done[base] == PASSES * group:
                     bank = sums.pop(base)
-                    size = min(width, C)
-                    for lo in range(0, width, size):
+                    size = min(group, C)
+                    for lo in range(0, group, size):
                         expert = (base + lo) // C
                         nc.scalar.activation(
                             y[:, base + lo : base + lo + size],
@@ -222,66 +206,72 @@ def tile_moe_pre_lin_relu2_kernel(
                             RELU,
                             bias=bias[:, expert : expert + 1],
                         )
-                    nc.scalar.activation(y[:, base : base + width], y[:, base : base + width], SQUARE)
+                    nc.scalar.activation(y[:, base : base + group], y[:, base : base + group], SQUARE)
 
+        panels = [(chunk, g) for chunk in range(CHUNKS) for g in range(PASSES)]
         load_tokens(0, 0)
         nc.sync.dma_start(slot_tokens[:], offs)
-        for lo, hi in zip(FIRST_CUTS[:-1], FIRST_CUTS[1:]):
-            load_gate(lo, hi)
+        load_tokens(0, 1)
+        nc.sync.dma_start(out=gate_cols[:], in_=gate[0, :].rearrange("(b p i) -> p b i", p=P, i=RUN))
+        for g, t in ((0, 2), (0, 3), (1, 0), (1, 1)):
+            load_tokens(g, t)
+        load_w(panels[0])
+        for g, t in ((1, 2), (1, 3), (2, 0)):
+            load_tokens(g, t)
+        load_w(panels[1])
         for t in range(1, PACK):
-            load_tokens(0, t)
-        first_raw = held.tile([P, HALF_E + 1, PACK * N], F32, name="x_f32_1", align_bytes=64)
-        load_w(0, range(HALF_E), first_raw[:, 0:HALF_E, :])
-        load_next_panel(0, first_raw[:, HALF_E:, :])
-        load_gate(CHUNK, SLOTS)
-        for t in range(PACK):
-            load_tokens(1, t)
+            load_tokens(2, t)
+        load_w(panels[2])
+        nc.sync.dma_start(out=bias[:], in_=b)
+        for r, pos in enumerate((pos1, pos2, pos3, pos4)):
+            nc.sync.dma_start(token_slots[r][:], pos)
 
-        round_w(0)
+        make_identity(nc, identity[:])
+        for block in range(GATE_BANKS):
+            spread_gate(block)
+
+        gather_x(0)
         for s in range(last + 1):
-            gather_x(s)
-            if s >= 1:
-                round_x(s - 1)
-                activate_finished()
-            if 1 <= s < len(panels) - 1:
-                free = held.tile([P, 1, PACK * N], F32, name="x_f32_%d" % ((s + 1) % 2), align_bytes=64)
-                load_next_panel(s, free)
-            if s == 1:
-                for t in range(PACK):
-                    load_tokens(2, t)
-                nc.sync.dma_start(out=bias[:], in_=b)
-                for r, pos in enumerate((pos1, pos2, pos3, pos4)):
-                    nc.sync.dma_start(token_slots[r][:], pos)
-            if s < len(panels) - 1:
-                round_w(s + 1)
-            if 1 <= s < last:
-                multiply_step(s - 1)
+            g, first, width = steps[s]
+            if s < last:
+                gather_x(s + 1)
+            gate_and_round(s)
+            if g == PASSES - 1:
+                for block in range(first // BANK, (first + width) // BANK):
+                    if block + GATE_BANKS < SLOTS // BANK:
+                        spread_gate(block + GATE_BANKS)
             if s == 0:
-                quantize_w(0)
-            if s < len(panels) - 1:
-                quantize_w(s + 1)
-
-        round_x(last)
-        late_codes = held.tile([P, PASSES - 1, C], U32, name="tokens2_2", align_bytes=64)
-        late_scales = held.tile([P, PASSES - 1, C], U8, name="late_scales", align_bytes=64)
-        for g in range(PASSES - 1):
-            quantize_and_multiply(g, LAST, C, late_bf[g][:], late_codes[:, g, :], late_scales[:, g, :])
-        for s in (last - 1, last):
-            multiply_step(s)
+                round_w(panels[0])
+            if s + 1 < len(panels):
+                round_w(panels[s + 1])
+            if s + 3 < len(panels):
+                load_w(panels[s + 3])
+            codes, scales = quantize_and_multiply(s)
+            if s == 0:
+                quantize_w(panels[0])
+            if s + 1 < len(panels):
+                quantize_w(panels[s + 1])
+            multiply(s, codes, scales)
             activate_finished()
 
-        partial = held.tile([P, TOP, T], F32, name="x_f32_%d" % ((last + 1) % 2), align_bytes=64)
+        picked = held.tile([P, 2, T], F32, name="picked")
+        pairs = held.tile([P, 2, T], F32, name="pairs")
+        total = held.tile([P, T], F32, name="total")
+        blocks = list(zip(TOKEN_CUTS[:-1], TOKEN_CUTS[1:]))
 
-        def combine(r, lo, hi):
-            offsets = token_slots[r][:, lo // STRIPE : hi // STRIPE]
-            if r == 0:
-                nc.vector.tensor_copy(partial[:, 0, lo:hi], y[:].indirect(offsets))
-            else:
-                nc.vector.tensor_tensor(partial[:, r, lo:hi], y[:].indirect(offsets), partial[:, r - 1, lo:hi], ADD)
+        def results(r, lo, hi):
+            return y[:].indirect(token_slots[r][:, lo // STRIPE : hi // STRIPE])
 
-        for r in range(TOP - 1):
-            for h in range(2):
-                combine(r, h * HALF, (h + 1) * HALF)
-        for queue, lo, hi in ((nc.sync, 0, HALF), (nc.scalar, HALF, T - LAST_STORE), (nc.sync, T - LAST_STORE, T)):
-            combine(TOP - 1, lo, hi)
-            queue.dma_start(out=out[:, lo:hi], in_=partial[:, TOP - 1, lo:hi])
+        def finish(i):
+            lo, hi = blocks[i]
+            nc.vector.tensor_tensor(total[:, lo:hi], pairs[:, 0, lo:hi], pairs[:, 1, lo:hi], ADD)
+            nc.sync.dma_start(out=out[:, lo:hi], in_=total[:, lo:hi])
+
+        for i, (lo, hi) in enumerate(blocks):
+            for r in range(2):
+                nc.scalar.activation(picked[:, r, lo:hi], results(r, lo, hi), COPY)
+            nc.vector.tensor_tensor(pairs[:, 0, lo:hi], results(2, lo, hi), picked[:, 0, lo:hi], ADD)
+            if i > 0:
+                finish(i - 1)
+            nc.vector.tensor_tensor(pairs[:, 1, lo:hi], results(3, lo, hi), picked[:, 1, lo:hi], ADD)
+        finish(len(blocks) - 1)

@@ -33,15 +33,17 @@ CHUNKS = E // CHUNK_E
 BANK = 512
 SPARE = 16
 RUN = 4
-GATE_BANKS = 3
-VECTOR_SHARE = 576
+GATE_BANKS = 4
+VECTOR_SHARE = 896
+CLOSING_SHARE = 256
 CLOSING_WIDTHS = (512, 256, 128, 128)
 TOKEN_CUTS = (0, 128, 384, 640, 896, 1024)
 LAST = (E - 1) * C
 
 
 def make_steps():
-    steps = [(g, chunk * CHUNK, CHUNK) for chunk in range(CHUNKS) for g in range(PASSES)][:-1]
+    steps = [(g, chunk * CHUNK, CHUNK) for g in range(PASSES) for chunk in range(2)]
+    steps = steps + [(g, chunk * CHUNK, CHUNK) for chunk in range(2, CHUNKS) for g in range(PASSES)][:-1]
     first = SLOTS - CHUNK
     for width in CLOSING_WIDTHS:
         steps.append((PASSES - 1, first, width))
@@ -51,11 +53,11 @@ def make_steps():
 
 def sum_of(slot):
     if slot >= LAST + C // 2:
-        return LAST + C // 2, C // 2, (SLOTS // BANK) % GATE_BANKS
+        return LAST + C // 2, C // 2, 1
     if slot >= LAST:
-        return LAST, C // 2, 7
+        return LAST, C // 2, 0
     if slot >= LAST - C:
-        return LAST - C, C, 6
+        return LAST - C, C, 7
     return slot - slot % BANK, BANK, GATE_BANKS + (slot // BANK) % 4
 
 
@@ -102,10 +104,14 @@ def tile_moe_pre_lin_relu2_kernel(
             nc.sync.dma_start(out=w_raw[key][:], in_=rows.rearrange("e (p t) n -> p e (t n)", t=PACK))
 
         def round_w(key):
-            w_bf[key] = two.tile([P, CHUNK_E * N, PACK], BF16, name="w_bf", align_bytes=64)
-            nc.vector.tensor_copy(
-                out=w_bf[key][:].rearrange("p (e c i) t -> p e c t i", e=CHUNK_E, i=RUN),
-                in_=w_raw[key][:].rearrange("p e (t c i) -> p e c t i", t=PACK, i=RUN),
+            w_bf[key] = held.tile([P, CHUNK_E * N, PACK], BF16, name="w_bf", align_bytes=64)
+            nc.gpsimd.tensor_scalar(
+                w_bf[key][:].rearrange("p (e n) t -> p e n t", e=CHUNK_E),
+                w_raw[key][:].rearrange("p e (t n) -> p e n t", t=PACK),
+                1.0,
+                0.0,
+                MULT,
+                ADD,
             )
 
         def quantize_w(key):
@@ -139,6 +145,8 @@ def tile_moe_pre_lin_relu2_kernel(
                     share = width // 2
                 elif t == 0 and width == CHUNK:
                     share = VECTOR_SHARE
+                elif t == 0 and width == CLOSING_WIDTHS[0]:
+                    share = CLOSING_SHARE
                 else:
                     share = 0
                 gather(s, t, share, width, False)
@@ -147,7 +155,7 @@ def tile_moe_pre_lin_relu2_kernel(
 
         def gate_and_round(s):
             g, first, width = steps[s]
-            x_bf[s] = two.tile([P, width, PACK], BF16, name="x_bf", align_bytes=64)
+            x_bf[s] = held.tile([P, width, PACK], BF16, name="x_bf", align_bytes=64)
             for lo in range(0, width, BANK):
                 n = min(BANK, width - lo)
                 block, start = divmod(first + lo, BANK)
@@ -208,20 +216,18 @@ def tile_moe_pre_lin_relu2_kernel(
                         )
                     nc.scalar.activation(y[:, base : base + group], y[:, base : base + group], SQUARE)
 
-        panels = [(chunk, g) for chunk in range(CHUNKS) for g in range(PASSES)]
+        panels = [panel(s) for s in range(CHUNKS * PASSES)]
         load_tokens(0, 0)
         nc.sync.dma_start(slot_tokens[:], offs)
         load_tokens(0, 1)
         nc.sync.dma_start(out=gate_cols[:], in_=gate[0, :].rearrange("(b p i) -> p b i", p=P, i=RUN))
-        for g, t in ((0, 2), (0, 3), (1, 0), (1, 1)):
-            load_tokens(g, t)
-        load_w(panels[0])
-        for g, t in ((1, 2), (1, 3), (2, 0)):
-            load_tokens(g, t)
-        load_w(panels[1])
-        for t in range(1, PACK):
-            load_tokens(2, t)
-        load_w(panels[2])
+        for t in range(2, PACK):
+            load_tokens(0, t)
+        for g in range(PASSES):
+            load_w(panels[g])
+            if g + 1 < PASSES:
+                for t in range(PACK):
+                    load_tokens(g + 1, t)
         nc.sync.dma_start(out=bias[:], in_=b)
         for r, pos in enumerate((pos1, pos2, pos3, pos4)):
             nc.sync.dma_start(token_slots[r][:], pos)
@@ -230,6 +236,7 @@ def tile_moe_pre_lin_relu2_kernel(
         for block in range(GATE_BANKS):
             spread_gate(block)
 
+        round_w(panels[0])
         gather_x(0)
         for s in range(last + 1):
             g, first, width = steps[s]
@@ -240,17 +247,13 @@ def tile_moe_pre_lin_relu2_kernel(
                 for block in range(first // BANK, (first + width) // BANK):
                     if block + GATE_BANKS < SLOTS // BANK:
                         spread_gate(block + GATE_BANKS)
-            if s == 0:
-                round_w(panels[0])
+            if s < len(panels):
+                quantize_w(panels[s])
             if s + 1 < len(panels):
                 round_w(panels[s + 1])
             if s + 3 < len(panels):
                 load_w(panels[s + 3])
             codes, scales = quantize_and_multiply(s)
-            if s == 0:
-                quantize_w(panels[0])
-            if s + 1 < len(panels):
-                quantize_w(panels[s + 1])
             multiply(s, codes, scales)
             activate_finished()
 

@@ -34,10 +34,12 @@ BANK = 512
 SPARE = 16
 RUN = 4
 GATE_BANKS = 4
-VECTOR_SHARE = 896
+VECTOR_SHARE = 832
+FIRST_SHARE = 608
 CLOSING_SHARE = 256
 CLOSING_WIDTHS = (512, 256, 128, 128)
-TOKEN_CUTS = (0, 128, 384, 640, 896, 1024)
+TOKEN_CUTS = (0, 256, 512, 768, 896, 1024)
+LISTS_ON_SCALAR = (1, 2, 3, 3, 2)
 LAST = (E - 1) * C
 
 
@@ -78,7 +80,10 @@ def tile_moe_pre_lin_relu2_kernel(
         token_slots = [held.tile([P, T // STRIPE], U16, name="token_slots%d" % r) for r in range(TOP)]
         bias = held.tile([P, E], F32, name="bias")
         identity = held.tile([P, P], F32, name="identity")
-        gate_cols = held.tile([P, SLOTS // BANK, RUN], F32, name="gate_cols")
+        gate_cols = [
+            held.tile([P, 2, RUN], F32, name="x_f32_1" if c == 1 else "gate_cols%d" % c, align_bytes=64)
+            for c in range(CHUNKS)
+        ]
         y = held.tile([P, SLOTS], F32, name="y")
         tokens = [
             [held.tile([P, T + SPARE], F32, name="tokens%d_%d" % (g, t), align_bytes=64) for t in range(PACK)]
@@ -97,36 +102,53 @@ def tile_moe_pre_lin_relu2_kernel(
         def load_tokens(g, t):
             nc.sync.dma_start(out=tokens[g][t][:, 0:T], in_=x_rows[g, t])
 
+        def load_gate(c):
+            row = gate[0, c * CHUNK : (c + 1) * CHUNK]
+            nc.sync.dma_start(out=gate_cols[c][:], in_=row.rearrange("(b p i) -> p b i", p=P, i=RUN))
+
         def load_w(key):
             chunk, g = key
-            w_raw[key] = three.tile([P, CHUNK_E, PACK * N], F32, name="w_raw", align_bytes=64)
+            pool, tag = (held, "w_raw_last") if key == panels[-1] else (three, "w_raw")
+            w_raw[key] = pool.tile([P, CHUNK_E, PACK * N], F32, name=tag, align_bytes=64)
             rows = w[chunk * CHUNK_E : (chunk + 1) * CHUNK_E, g * K_PASS : (g + 1) * K_PASS, :]
             nc.sync.dma_start(out=w_raw[key][:], in_=rows.rearrange("e (p t) n -> p e (t n)", t=PACK))
 
-        def round_w(key):
-            w_bf[key] = held.tile([P, CHUNK_E * N, PACK], BF16, name="w_bf", align_bytes=64)
-            nc.gpsimd.tensor_scalar(
-                w_bf[key][:].rearrange("p (e n) t -> p e n t", e=CHUNK_E),
-                w_raw[key][:].rearrange("p e (t n) -> p e n t", t=PACK),
-                1.0,
-                0.0,
-                MULT,
-                ADD,
-            )
+        def w_parts(s):
+            parts = [(panels[s], 0, CHUNK_E)]
+            early = s - (len(panels) - 1 - CHUNK_E)
+            if early >= 0:
+                parts.append((panels[-1], early, 1))
+            return parts
 
-        def quantize_w(key):
-            w_codes[key] = three.tile([P, CHUNK_E * N], U32, name="w_codes", align_bytes=64)
-            w_scales[key] = three.tile([P, CHUNK_E * N], U8, name="w_scales", align_bytes=64)
-            nc.vector.quantize_mx(
-                out=w_codes[key][:].bitcast(FP8X4),
-                scales=w_scales[key][:],
-                in_=w_bf[key][:].rearrange("p n t -> p (n t)"),
-            )
+        def round_w(s):
+            parts = w_parts(s)
+            w_bf[s] = held.tile([P, sum(n for key, e, n in parts) * N, PACK], BF16, name="w_bf", align_bytes=64)
+            for i, (key, e, n) in enumerate(parts):
+                nc.gpsimd.tensor_scalar(
+                    w_bf[s][:, i * CHUNK_E * N : (i * CHUNK_E + n) * N, :].rearrange("p (e n) t -> p e n t", n=N),
+                    w_raw[key][:, e : e + n, :].rearrange("p e (t n) -> p e n t", t=PACK),
+                    1.0,
+                    0.0,
+                    MULT,
+                    ADD,
+                )
+
+        def quantize_w(s):
+            for i, (key, e, n) in enumerate(w_parts(s)):
+                if e == 0:
+                    pool, tag = (held, "_last") if key == panels[-1] else (three, "")
+                    w_codes[key] = pool.tile([P, CHUNK_E * N], U32, name="w_codes" + tag, align_bytes=64)
+                    w_scales[key] = pool.tile([P, CHUNK_E * N], U8, name="w_scales" + tag, align_bytes=64)
+                nc.vector.quantize_mx(
+                    out=w_codes[key][:, e * N : (e + n) * N].bitcast(FP8X4),
+                    scales=w_scales[key][:, e * N : (e + n) * N],
+                    in_=w_bf[s][:, i * CHUNK_E * N : (i * CHUNK_E + n) * N, :].rearrange("p n t -> p (n t)"),
+                )
 
         def spread_gate(block):
             gate_rows[block] = psum.tile([P, RUN, P], F32, name="bank%d" % (block % GATE_BANKS))
             for i in range(RUN):
-                column = gate_cols[:, block, i : i + 1].to_broadcast([P, P])
+                column = gate_cols[block // 2][:, block % 2, i : i + 1].to_broadcast([P, P])
                 nc.tensor.transpose(gate_rows[block][:, i, :], column, identity[:])
 
         def gather(s, t, lo, hi, on_vector):
@@ -139,10 +161,10 @@ def tile_moe_pre_lin_relu2_kernel(
 
         def gather_x(s):
             g, first, width = steps[s]
-            x_f32[s] = three.tile([P, PACK, width], F32, name="x_f32", align_bytes=64)
+            x_f32[s] = held.tile([P, PACK, width], F32, name="x_f32_%d" % (s % 3), align_bytes=64)
             for t in range(PACK):
                 if s == 0:
-                    share = width // 2
+                    share = FIRST_SHARE
                 elif t == 0 and width == CHUNK:
                     share = VECTOR_SHARE
                 elif t == 0 and width == CLOSING_WIDTHS[0]:
@@ -220,14 +242,20 @@ def tile_moe_pre_lin_relu2_kernel(
         load_tokens(0, 0)
         nc.sync.dma_start(slot_tokens[:], offs)
         load_tokens(0, 1)
-        nc.sync.dma_start(out=gate_cols[:], in_=gate[0, :].rearrange("(b p i) -> p b i", p=P, i=RUN))
+        load_gate(0)
         for t in range(2, PACK):
             load_tokens(0, t)
-        for g in range(PASSES):
-            load_w(panels[g])
-            if g + 1 < PASSES:
-                for t in range(PACK):
-                    load_tokens(g + 1, t)
+        load_gate(1)
+        load_w(panels[0])
+        for g in range(1, PASSES):
+            for t in range(PACK):
+                load_tokens(g, t)
+            if g == 1:
+                load_w(panels[1])
+                load_w(panels[2])
+        load_gate(2)
+        load_gate(3)
+        load_w(panels[-1])
         nc.sync.dma_start(out=bias[:], in_=b)
         for r, pos in enumerate((pos1, pos2, pos3, pos4)):
             nc.sync.dma_start(token_slots[r][:], pos)
@@ -236,7 +264,7 @@ def tile_moe_pre_lin_relu2_kernel(
         for block in range(GATE_BANKS):
             spread_gate(block)
 
-        round_w(panels[0])
+        round_w(0)
         gather_x(0)
         for s in range(last + 1):
             g, first, width = steps[s]
@@ -247,34 +275,40 @@ def tile_moe_pre_lin_relu2_kernel(
                 for block in range(first // BANK, (first + width) // BANK):
                     if block + GATE_BANKS < SLOTS // BANK:
                         spread_gate(block + GATE_BANKS)
-            if s < len(panels):
-                quantize_w(panels[s])
-            if s + 1 < len(panels):
-                round_w(panels[s + 1])
-            if s + 3 < len(panels):
+            if s < len(panels) - 1:
+                quantize_w(s)
+            if s + 1 < len(panels) - 1:
+                round_w(s + 1)
+            if s + 3 < len(panels) - 1:
                 load_w(panels[s + 3])
             codes, scales = quantize_and_multiply(s)
             multiply(s, codes, scales)
             activate_finished()
 
-        picked = held.tile([P, 2, T], F32, name="picked")
+        picked = held.tile([P, TOP - 1, T], F32, name="picked")
         pairs = held.tile([P, 2, T], F32, name="pairs")
         total = held.tile([P, T], F32, name="total")
-        blocks = list(zip(TOKEN_CUTS[:-1], TOKEN_CUTS[1:]))
+        blocks = [slice(lo, hi) for lo, hi in zip(TOKEN_CUTS[:-1], TOKEN_CUTS[1:])]
+        final = len(blocks) - 1
 
-        def results(r, lo, hi):
-            return y[:].indirect(token_slots[r][:, lo // STRIPE : hi // STRIPE])
+        def results(r, cols):
+            return y[:].indirect(token_slots[r][:, cols.start // STRIPE : cols.stop // STRIPE])
 
-        def finish(i):
-            lo, hi = blocks[i]
-            nc.vector.tensor_tensor(total[:, lo:hi], pairs[:, 0, lo:hi], pairs[:, 1, lo:hi], ADD)
-            nc.sync.dma_start(out=out[:, lo:hi], in_=total[:, lo:hi])
+        def finish(i, queue):
+            cols = blocks[i]
+            nc.vector.tensor_tensor(total[:, cols], pairs[:, 0, cols], pairs[:, 1, cols], ADD)
+            queue.dma_start(out=out[:, cols], in_=total[:, cols])
 
-        for i, (lo, hi) in enumerate(blocks):
-            for r in range(2):
-                nc.scalar.activation(picked[:, r, lo:hi], results(r, lo, hi), COPY)
-            nc.vector.tensor_tensor(pairs[:, 0, lo:hi], results(2, lo, hi), picked[:, 0, lo:hi], ADD)
-            if i > 0:
-                finish(i - 1)
-            nc.vector.tensor_tensor(pairs[:, 1, lo:hi], results(3, lo, hi), picked[:, 1, lo:hi], ADD)
-        finish(len(blocks) - 1)
+        for i, cols in enumerate(blocks):
+            on_scalar = LISTS_ON_SCALAR[i]
+            for r in range(on_scalar):
+                nc.scalar.activation(picked[:, r, cols], results(r, cols), COPY)
+            if on_scalar == 1:
+                nc.vector.tensor_copy(picked[:, 1, cols], results(1, cols))
+            nc.vector.tensor_tensor(pairs[:, 0, cols], results(3, cols), picked[:, 0, cols], ADD)
+            if 0 < i < final:
+                finish(i - 1, nc.sync)
+            third = picked[:, 2, cols] if on_scalar == 3 else results(2, cols)
+            nc.vector.tensor_tensor(pairs[:, 1, cols], third, picked[:, 1, cols], ADD)
+        finish(final - 1, nc.scalar)
+        finish(final, nc.sync)

@@ -34,9 +34,9 @@ BANK = 512
 SPARE = 16
 RUN = 4
 GATE_BANKS = 4
-VECTOR_SHARE = 832
+VECTOR_SHARE = 928
 FIRST_SHARE = 608
-CLOSING_SHARE = 256
+CLOSING_SHARE = 320
 CLOSING_WIDTHS = (512, 256, 128, 128)
 TOKEN_CUTS = (0, 256, 512, 768, 896, 1024)
 LISTS_ON_SCALAR = (1, 2, 3, 3, 2)
@@ -172,8 +172,13 @@ def tile_moe_pre_lin_relu2_kernel(
                 else:
                     share = 0
                 gather(s, t, share, width, False)
-                if share:
+                if share and s == 0:
                     gather(s, t, 0, share, True)
+
+        def gather_share(s):
+            share = {CHUNK: VECTOR_SHARE, CLOSING_WIDTHS[0]: CLOSING_SHARE}.get(steps[s][2])
+            if share:
+                gather(s, 0, 0, share, True)
 
         def gate_and_round(s):
             g, first, width = steps[s]
@@ -271,17 +276,19 @@ def tile_moe_pre_lin_relu2_kernel(
             if s < last:
                 gather_x(s + 1)
             gate_and_round(s)
+            if s < last:
+                gather_share(s + 1)
             if g == PASSES - 1:
                 for block in range(first // BANK, (first + width) // BANK):
                     if block + GATE_BANKS < SLOTS // BANK:
                         spread_gate(block + GATE_BANKS)
+            codes, scales = quantize_and_multiply(s)
             if s < len(panels) - 1:
                 quantize_w(s)
             if s + 1 < len(panels) - 1:
                 round_w(s + 1)
             if s + 3 < len(panels) - 1:
                 load_w(panels[s + 3])
-            codes, scales = quantize_and_multiply(s)
             multiply(s, codes, scales)
             activate_finished()
 

@@ -18,6 +18,7 @@ U8 = mybir.dt.uint8
 FP8X4 = mybir.dt.float8_e4m3fn_x4
 MULT = mybir.AluOpType.mult
 ADD = mybir.AluOpType.add
+MAX = mybir.AluOpType.max
 COPY = mybir.ActivationFunctionType.Copy
 RELU = mybir.ActivationFunctionType.Relu
 SQUARE = mybir.ActivationFunctionType.Square
@@ -30,17 +31,21 @@ STRIPE = 16
 CHUNK_E = 4
 CHUNK = CHUNK_E * C
 CHUNKS = E // CHUNK_E
+FULL_STEPS = CHUNKS * PASSES - 1
 BANK = 512
+GATE_BANKS = 4
 SPARE = 16
 RUN = 4
-GATE_BANKS = 4
-VECTOR_SHARE = 928
-FIRST_SHARE = 608
-CLOSING_SHARE = 320
+X_BUFFERS = 3
 CLOSING_WIDTHS = (512, 256, 128, 128)
+LAST = (E - 1) * C
+VECTOR_SHARE = 960
+CLOSING_SHARE = 320
+POOL_SHARE = 96
+CLOSING_POOL_SHARE = 160
+FIRST_EARLY = FULL_STEPS - 1 - CHUNK_E
 TOKEN_CUTS = (0, 256, 512, 768, 896, 1024)
 LISTS_ON_SCALAR = (1, 2, 3, 3, 2)
-LAST = (E - 1) * C
 
 
 def make_steps():
@@ -54,13 +59,13 @@ def make_steps():
 
 
 def sum_of(slot):
-    if slot >= LAST + C // 2:
-        return LAST + C // 2, C // 2, 1
     if slot >= LAST:
-        return LAST, C // 2, 0
+        half = (slot - LAST) // (C // 2)
+        return LAST + half * (C // 2), C // 2, half
+    bank = GATE_BANKS + (slot // BANK) % GATE_BANKS
     if slot >= LAST - C:
-        return LAST - C, C, 7
-    return slot - slot % BANK, BANK, GATE_BANKS + (slot // BANK) % 4
+        return LAST - C, C, bank
+    return slot - slot % BANK, BANK, bank
 
 
 def tile_moe_pre_lin_relu2_kernel(
@@ -69,6 +74,10 @@ def tile_moe_pre_lin_relu2_kernel(
     nc = tc.nc
     steps = make_steps()
     last = len(steps) - 1
+    panels = [(first // CHUNK, g) for g, first, width in steps]
+    last_panel = panels[last]
+    pooled = {s: POOL_SHARE for s in range(FIRST_EARLY)}
+    pooled[FULL_STEPS] = CLOSING_POOL_SHARE
 
     with ExitStack() as ctx:
         held = ctx.enter_context(tc.tile_pool(name="held", bufs=1))
@@ -81,9 +90,11 @@ def tile_moe_pre_lin_relu2_kernel(
         bias = held.tile([P, E], F32, name="bias")
         identity = held.tile([P, P], F32, name="identity")
         gate_cols = [
-            held.tile([P, 2, RUN], F32, name="x_f32_1" if c == 1 else "gate_cols%d" % c, align_bytes=64)
+            held.tile([P, CHUNK // BANK, RUN], F32, name="x_f32_1" if c == 1 else "gate_cols%d" % c, align_bytes=64)
             for c in range(CHUNKS)
         ]
+        gate_early = held.tile([P, 2, POOL_SHARE], F32, name="gate_early")
+        gate_closing = held.tile([P, CLOSING_POOL_SHARE], F32, name="gate_closing")
         y = held.tile([P, SLOTS], F32, name="y")
         tokens = [
             [held.tile([P, T + SPARE], F32, name="tokens%d_%d" % (g, t), align_bytes=64) for t in range(PACK)]
@@ -92,41 +103,36 @@ def tile_moe_pre_lin_relu2_kernel(
         x_rows = xT.rearrange("(g p t) c -> g t p c", g=PASSES, t=PACK)
 
         w_raw, w_bf, w_codes, w_scales = {}, {}, {}, {}
-        x_f32, x_bf, gate_rows = {}, {}, {}
-        sums, done = {}, {}
-
-        def panel(s):
-            g, first, width = steps[s]
-            return first // CHUNK, g
+        x_f32, x_bf, x_codes, x_scales = {}, {}, {}, {}
+        gate_rows, sums, done = {}, {}, {}
 
         def load_tokens(g, t):
             nc.sync.dma_start(out=tokens[g][t][:, 0:T], in_=x_rows[g, t])
 
-        def load_gate(c):
+        def load_gate_cols(c):
             row = gate[0, c * CHUNK : (c + 1) * CHUNK]
-            nc.sync.dma_start(out=gate_cols[c][:], in_=row.rearrange("(b p i) -> p b i", p=P, i=RUN))
+            nc.sync.dma_start(out=gate_cols[c][:], in_=row.rearrange("(h p i) -> p h i", p=P, i=RUN))
 
-        def load_w(key):
-            chunk, g = key
-            pool, tag = (held, "w_raw_last") if key == panels[-1] else (three, "w_raw")
-            w_raw[key] = pool.tile([P, CHUNK_E, PACK * N], F32, name=tag, align_bytes=64)
+        def load_w(panel):
+            chunk, g = panel
+            pool, tag = (held, "w_raw_last") if panel == last_panel else (three, "w_raw")
+            w_raw[panel] = pool.tile([P, CHUNK_E, PACK * N], F32, name=tag, align_bytes=64)
             rows = w[chunk * CHUNK_E : (chunk + 1) * CHUNK_E, g * K_PASS : (g + 1) * K_PASS, :]
-            nc.sync.dma_start(out=w_raw[key][:], in_=rows.rearrange("e (p t) n -> p e (t n)", t=PACK))
+            nc.sync.dma_start(out=w_raw[panel][:], in_=rows.rearrange("e (p t) n -> p e (t n)", t=PACK))
 
         def w_parts(s):
             parts = [(panels[s], 0, CHUNK_E)]
-            early = s - (len(panels) - 1 - CHUNK_E)
-            if early >= 0:
-                parts.append((panels[-1], early, 1))
+            if FIRST_EARLY <= s < FIRST_EARLY + CHUNK_E:
+                parts.append((last_panel, s - FIRST_EARLY, 1))
             return parts
 
         def round_w(s):
             parts = w_parts(s)
-            w_bf[s] = held.tile([P, sum(n for key, e, n in parts) * N, PACK], BF16, name="w_bf", align_bytes=64)
-            for i, (key, e, n) in enumerate(parts):
+            w_bf[s] = held.tile([P, sum(n for panel, e, n in parts) * N, PACK], BF16, name="w_bf", align_bytes=64)
+            for i, (panel, e, n) in enumerate(parts):
                 nc.gpsimd.tensor_scalar(
                     w_bf[s][:, i * CHUNK_E * N : (i * CHUNK_E + n) * N, :].rearrange("p (e n) t -> p e n t", n=N),
-                    w_raw[key][:, e : e + n, :].rearrange("p e (t n) -> p e n t", t=PACK),
+                    w_raw[panel][:, e : e + n, :].rearrange("p e (t n) -> p e n t", t=PACK),
                     1.0,
                     0.0,
                     MULT,
@@ -134,76 +140,81 @@ def tile_moe_pre_lin_relu2_kernel(
                 )
 
         def quantize_w(s):
-            for i, (key, e, n) in enumerate(w_parts(s)):
+            for i, (panel, e, n) in enumerate(w_parts(s)):
                 if e == 0:
-                    pool, tag = (held, "_last") if key == panels[-1] else (three, "")
-                    w_codes[key] = pool.tile([P, CHUNK_E * N], U32, name="w_codes" + tag, align_bytes=64)
-                    w_scales[key] = pool.tile([P, CHUNK_E * N], U8, name="w_scales" + tag, align_bytes=64)
+                    pool, tag = (held, "_last") if panel == last_panel else (three, "")
+                    w_codes[panel] = pool.tile([P, CHUNK_E * N], U32, name="w_codes" + tag, align_bytes=64)
+                    w_scales[panel] = pool.tile([P, CHUNK_E * N], U8, name="w_scales" + tag, align_bytes=64)
                 nc.vector.quantize_mx(
-                    out=w_codes[key][:, e * N : (e + n) * N].bitcast(FP8X4),
-                    scales=w_scales[key][:, e * N : (e + n) * N],
+                    out=w_codes[panel][:, e * N : (e + n) * N].bitcast(FP8X4),
+                    scales=w_scales[panel][:, e * N : (e + n) * N],
                     in_=w_bf[s][:, i * CHUNK_E * N : (i * CHUNK_E + n) * N, :].rearrange("p n t -> p (n t)"),
                 )
 
         def spread_gate(block):
             gate_rows[block] = psum.tile([P, RUN, P], F32, name="bank%d" % (block % GATE_BANKS))
+            chunk, h = divmod(block, CHUNK // BANK)
             for i in range(RUN):
-                column = gate_cols[block // 2][:, block % 2, i : i + 1].to_broadcast([P, P])
+                column = gate_cols[chunk][:, h, i : i + 1].to_broadcast([P, P])
                 nc.tensor.transpose(gate_rows[block][:, i, :], column, identity[:])
 
-        def gather(s, t, lo, hi, on_vector):
+        def window(s, t, lo, hi):
             g, first, width = steps[s]
-            window = tokens[g][t][:].indirect(slot_tokens[:, (first + lo) // STRIPE : (first + hi) // STRIPE])
-            if on_vector:
-                nc.vector.tensor_copy(x_f32[s][:, t, lo:hi], window)
-            else:
-                nc.scalar.activation(x_f32[s][:, t, lo:hi], window, COPY)
+            return tokens[g][t][:].indirect(slot_tokens[:, (first + lo) // STRIPE : (first + hi) // STRIPE])
 
-        def gather_x(s):
-            g, first, width = steps[s]
-            x_f32[s] = held.tile([P, PACK, width], F32, name="x_f32_%d" % (s % 3), align_bytes=64)
+        def vector_share(s, t):
+            if s == 0:
+                return CHUNK // 2
+            if t == 0 and s <= FULL_STEPS:
+                return VECTOR_SHARE if s < FULL_STEPS else CLOSING_SHARE
+            return 0
+
+        def gather_on_scalar(s, t):
+            share, width = vector_share(s, t), steps[s][2]
+            nc.scalar.activation(x_f32[s][:, t, share:width], window(s, t, share, width), COPY)
+
+        def gather_on_vector(s, t):
+            share = vector_share(s, t)
+            nc.vector.tensor_copy(x_f32[s][:, t, 0:share], window(s, t, 0, share))
+
+        def open_step(s):
+            x_f32[s] = held.tile([P, PACK, steps[s][2]], F32, name="x_f32_%d" % (s % X_BUFFERS), align_bytes=64)
             for t in range(PACK):
+                gather_on_scalar(s, t)
                 if s == 0:
-                    share = FIRST_SHARE
-                elif t == 0 and width == CHUNK:
-                    share = VECTOR_SHARE
-                elif t == 0 and width == CLOSING_WIDTHS[0]:
-                    share = CLOSING_SHARE
-                else:
-                    share = 0
-                gather(s, t, share, width, False)
-                if share and s == 0:
-                    gather(s, t, 0, share, True)
+                    gather_on_vector(s, t)
 
-        def gather_share(s):
-            share = {CHUNK: VECTOR_SHARE, CLOSING_WIDTHS[0]: CLOSING_SHARE}.get(steps[s][2])
-            if share:
-                gather(s, 0, 0, share, True)
+        def times_gate(engine, s, lo, hi, rows):
+            engine.tensor_tensor(
+                x_bf[s][:, lo:hi, :].rearrange("p (c i) t -> p c t i", i=RUN),
+                x_f32[s][:, :, lo:hi].rearrange("p t (c i) -> p c t i", i=RUN),
+                rows.unsqueeze(2).to_broadcast([P, (hi - lo) // RUN, PACK, RUN]),
+                MULT,
+            )
 
         def gate_and_round(s):
             g, first, width = steps[s]
-            x_bf[s] = held.tile([P, width, PACK], BF16, name="x_bf", align_bytes=64)
-            for lo in range(0, width, BANK):
-                n = min(BANK, width - lo)
-                block, start = divmod(first + lo, BANK)
-                rows = gate_rows[block][:, :, start // RUN : (start + n) // RUN].rearrange("p i c -> p c i")
-                nc.vector.tensor_tensor(
-                    x_bf[s][:, lo : lo + n, :].rearrange("p (c i) t -> p c t i", i=RUN),
-                    x_f32[s][:, :, lo : lo + n].rearrange("p t (c i) -> p c t i", i=RUN),
-                    rows.unsqueeze(2).to_broadcast([P, n // RUN, PACK, RUN]),
-                    MULT,
-                )
+            tag = "x_bf" if s <= FULL_STEPS else "x_bf%d" % s
+            x_bf[s] = held.tile([P, width, PACK], BF16, name=tag, align_bytes=64)
+            m = pooled.get(s, 0)
+            if m:
+                rows = gate_closing[:] if s == FULL_STEPS else gate_early[:, first // CHUNK, :]
+                times_gate(nc.gpsimd, s, 0, m, rows.rearrange("p (c i) -> p c i", i=RUN))
+            for start in range(0, width, BANK):
+                lo, hi = max(start, m), min(start + BANK, width)
+                block, col = divmod(first + lo, BANK)
+                rows = gate_rows[block][:, :, col // RUN : (col + hi - lo) // RUN]
+                times_gate(nc.vector, s, lo, hi, rows.rearrange("p i c -> p c i"))
 
-        def quantize_and_multiply(s):
-            g, first, width = steps[s]
-            codes = two.tile([P, width], U32, name="x_codes", align_bytes=64)
-            scales = two.tile([P, width], U8, name="x_scales", align_bytes=64)
+        def quantize_x(s):
+            width = steps[s][2]
+            x_codes[s] = two.tile([P, width], U32, name="x_codes", align_bytes=64)
+            x_scales[s] = two.tile([P, width], U8, name="x_scales", align_bytes=64)
             nc.vector.quantize_mx(
-                out=codes[:].bitcast(FP8X4), scales=scales[:], in_=x_bf[s][:].rearrange("p c t -> p (c t)")
+                out=x_codes[s][:].bitcast(FP8X4), scales=x_scales[s][:], in_=x_bf[s][:].rearrange("p c t -> p (c t)")
             )
-            return codes, scales
 
-        def multiply(s, codes, scales):
+        def multiply(s):
             g, first, width = steps[s]
             lo = first
             while lo < first + width:
@@ -217,10 +228,10 @@ def tile_moe_pre_lin_relu2_kernel(
                 x_cols = slice(lo - first, lo - first + size)
                 nc.tensor.matmul_mx(
                     out=sums[base][:, lo - base : lo - base + size],
-                    lhsT=w_codes[panel(s)][:, w_cols].bitcast(FP8X4),
-                    lhsT_scale=w_scales[panel(s)][:, w_cols],
-                    rhs=codes[:, x_cols].bitcast(FP8X4),
-                    rhs_scale=scales[:, x_cols],
+                    lhsT=w_codes[panels[s]][:, w_cols].bitcast(FP8X4),
+                    lhsT_scale=w_scales[panels[s]][:, w_cols],
+                    rhs=x_codes[s][:, x_cols].bitcast(FP8X4),
+                    rhs_scale=x_scales[s][:, x_cols],
                     start=(done[base] == 0),
                     stop=(done[base] + size == PASSES * group),
                 )
@@ -230,7 +241,7 @@ def tile_moe_pre_lin_relu2_kernel(
         def activate_finished():
             for base in sorted(sums):
                 group = sum_of(base)[1]
-                if done[base] == PASSES * group:
+                if done[base] == PASSES * group and base < LAST:
                     bank = sums.pop(base)
                     size = min(group, C)
                     for lo in range(0, group, size):
@@ -243,24 +254,25 @@ def tile_moe_pre_lin_relu2_kernel(
                         )
                     nc.scalar.activation(y[:, base : base + group], y[:, base : base + group], SQUARE)
 
-        panels = [panel(s) for s in range(CHUNKS * PASSES)]
         load_tokens(0, 0)
         nc.sync.dma_start(slot_tokens[:], offs)
         load_tokens(0, 1)
-        load_gate(0)
+        load_gate_cols(0)
         for t in range(2, PACK):
             load_tokens(0, t)
-        load_gate(1)
+        load_gate_cols(1)
+        nc.sync.dma_start(out=gate_early[:], in_=gate[0:P, :].rearrange("p (c j) -> p c j", c=CHUNKS)[:, 0:2, 0:POOL_SHARE])
         load_w(panels[0])
-        for g in range(1, PASSES):
-            for t in range(PACK):
-                load_tokens(g, t)
-            if g == 1:
-                load_w(panels[1])
-                load_w(panels[2])
-        load_gate(2)
-        load_gate(3)
-        load_w(panels[-1])
+        for t in range(PACK):
+            load_tokens(1, t)
+        load_w(panels[1])
+        load_w(panels[2])
+        for t in range(PACK):
+            load_tokens(2, t)
+        for c in range(2, CHUNKS):
+            load_gate_cols(c)
+        nc.sync.dma_start(out=gate_closing[:], in_=gate[0:P, SLOTS - CHUNK : SLOTS - CHUNK + CLOSING_POOL_SHARE])
+        load_w(last_panel)
         nc.sync.dma_start(out=bias[:], in_=b)
         for r, pos in enumerate((pos1, pos2, pos3, pos4)):
             nc.sync.dma_start(token_slots[r][:], pos)
@@ -270,27 +282,38 @@ def tile_moe_pre_lin_relu2_kernel(
             spread_gate(block)
 
         round_w(0)
-        gather_x(0)
-        for s in range(last + 1):
+        open_step(0)
+        for s in range(FULL_STEPS):
             g, first, width = steps[s]
-            if s < last:
-                gather_x(s + 1)
+            open_step(s + 1)
             gate_and_round(s)
-            if s < last:
-                gather_share(s + 1)
-            if g == PASSES - 1:
+            gather_on_vector(s + 1, 0)
+            if g == PASSES - 1 and first < 2 * CHUNK:
                 for block in range(first // BANK, (first + width) // BANK):
-                    if block + GATE_BANKS < SLOTS // BANK:
-                        spread_gate(block + GATE_BANKS)
-            codes, scales = quantize_and_multiply(s)
-            if s < len(panels) - 1:
-                quantize_w(s)
-            if s + 1 < len(panels) - 1:
+                    spread_gate(block + GATE_BANKS)
+            quantize_x(s)
+            quantize_w(s)
+            if s + 1 < FULL_STEPS:
                 round_w(s + 1)
-            if s + 3 < len(panels) - 1:
+            if s + 3 < FULL_STEPS:
                 load_w(panels[s + 3])
-            multiply(s, codes, scales)
+            multiply(s)
             activate_finished()
+
+        for s in range(FULL_STEPS, last + 1):
+            if s < last:
+                open_step(s + 1)
+            gate_and_round(s)
+            for ready in ([s - 1] if s > FULL_STEPS else []) + ([s] if s == last else []):
+                quantize_x(ready)
+                multiply(ready)
+                activate_finished()
+
+        halves = [(base, y[:, base : base + C // 2]) for base in sorted(sums)]
+        for base, half in halves:
+            nc.vector.tensor_scalar(half, sums[base][:], bias[:, E - 1 : E], 0.0, ADD, MAX)
+        for base, half in halves:
+            nc.vector.tensor_tensor(half, half, half, MULT)
 
         picked = held.tile([P, TOP - 1, T], F32, name="picked")
         pairs = held.tile([P, 2, T], F32, name="pairs")

@@ -254,6 +254,10 @@ def tile_moe_pre_lin_relu2_kernel(
                         )
                     nc.scalar.activation(y[:, base : base + group], y[:, base : base + group], SQUARE)
 
+        unread = held.tile([P, 2], F32, name="unread")
+        nc.vector.memset(unread[:, 0:1], 0.0)
+        nc.scalar.activation(unread[:, 1:2], unread[:, 0:1], RELU)
+
         load_tokens(0, 0)
         nc.sync.dma_start(slot_tokens[:], offs)
         load_tokens(0, 1)

@@ -290,15 +290,15 @@ def tile_moe_pre_lin_relu2_kernel(
         for s in range(FULL_STEPS):
             g, first, width = steps[s]
             open_step(s + 1)
-            gate_and_round(s)
             gather_on_vector(s + 1, 0)
+            gate_and_round(s)
             if g == PASSES - 1 and first < 2 * CHUNK:
                 for block in range(first // BANK, (first + width) // BANK):
                     spread_gate(block + GATE_BANKS)
-            quantize_x(s)
             quantize_w(s)
             if s + 1 < FULL_STEPS:
                 round_w(s + 1)
+            quantize_x(s)
             if s + 3 < FULL_STEPS:
                 load_w(panels[s + 3])
             multiply(s)

@@ -39,11 +39,14 @@ RUN = 4
 X_BUFFERS = 3
 CLOSING_WIDTHS = (512, 256, 128, 128)
 LAST = (E - 1) * C
-VECTOR_SHARE = 960
-CLOSING_SHARE = 320
-POOL_SHARE = 96
+PAIR = 2
+VECTOR_SHARE = CHUNK
+HEAD_SHARE = 1536
+CLOSING_SHARE = 512
+POOL_SHARE = 208
+HEAD_POOL_SHARE = 288
+LATE_POOL_SHARE = 128
 CLOSING_POOL_SHARE = 160
-FIRST_EARLY = FULL_STEPS - 1 - CHUNK_E
 TOKEN_CUTS = (0, 256, 512, 768, 896, 1024)
 LISTS_ON_SCALAR = (1, 2, 3, 3, 2)
 
@@ -75,9 +78,16 @@ def tile_moe_pre_lin_relu2_kernel(
     steps = make_steps()
     last = len(steps) - 1
     panels = [(first // CHUNK, g) for g, first, width in steps]
-    last_panel = panels[last]
-    pooled = {s: POOL_SHARE for s in range(FIRST_EARLY)}
+    pooled = {s: POOL_SHARE for s in range(FULL_STEPS)}
+    pooled[0] = HEAD_POOL_SHARE
+    pooled[FULL_STEPS - 2] = LATE_POOL_SHARE
+    pooled[FULL_STEPS - 1] = LATE_POOL_SHARE
     pooled[FULL_STEPS] = CLOSING_POOL_SHARE
+    shares = {s: VECTOR_SHARE for s in range(FULL_STEPS)}
+    shares[1] = HEAD_SHARE
+    shares[FULL_STEPS] = CLOSING_SHARE
+    shares[FULL_STEPS + 1] = CLOSING_SHARE
+    pooled_of_chunk = [max(m for s, m in pooled.items() if panels[s][0] == c) for c in range(CHUNKS)]
 
     with ExitStack() as ctx:
         held = ctx.enter_context(tc.tile_pool(name="held", bufs=1))
@@ -93,8 +103,7 @@ def tile_moe_pre_lin_relu2_kernel(
             held.tile([P, CHUNK // BANK, RUN], F32, name="x_f32_1" if c == 1 else "gate_cols%d" % c, align_bytes=64)
             for c in range(CHUNKS)
         ]
-        gate_early = held.tile([P, 2, POOL_SHARE], F32, name="gate_early")
-        gate_closing = held.tile([P, CLOSING_POOL_SHARE], F32, name="gate_closing")
+        gate_pool = [held.tile([P, pooled_of_chunk[c]], F32, name="gate_pool%d" % c) for c in range(CHUNKS)]
         y = held.tile([P, SLOTS], F32, name="y")
         tokens = [
             [held.tile([P, T + SPARE], F32, name="tokens%d_%d" % (g, t), align_bytes=64) for t in range(PACK)]
@@ -113,43 +122,40 @@ def tile_moe_pre_lin_relu2_kernel(
             row = gate[0, c * CHUNK : (c + 1) * CHUNK]
             nc.sync.dma_start(out=gate_cols[c][:], in_=row.rearrange("(h p i) -> p h i", p=P, i=RUN))
 
-        def load_w(panel):
-            chunk, g = panel
-            pool, tag = (held, "w_raw_last") if panel == last_panel else (three, "w_raw")
-            w_raw[panel] = pool.tile([P, CHUNK_E, PACK * N], F32, name=tag, align_bytes=64)
+        def load_gate_pool(c):
+            nc.sync.dma_start(out=gate_pool[c][:], in_=gate[0:P, c * CHUNK : c * CHUNK + pooled_of_chunk[c]])
+
+        def load_w(s):
+            chunk, g = panels[s]
+            w_raw[s] = three.tile([P, CHUNK_E, PACK * N], F32, name="w_raw", align_bytes=64)
             rows = w[chunk * CHUNK_E : (chunk + 1) * CHUNK_E, g * K_PASS : (g + 1) * K_PASS, :]
-            nc.sync.dma_start(out=w_raw[panel][:], in_=rows.rearrange("e (p t) n -> p e (t n)", t=PACK))
+            nc.sync.dma_start(out=w_raw[s][:], in_=rows.rearrange("e (p t) n -> p e (t n)", t=PACK))
 
-        def w_parts(s):
-            parts = [(panels[s], 0, CHUNK_E)]
-            if FIRST_EARLY <= s < FIRST_EARLY + CHUNK_E:
-                parts.append((last_panel, s - FIRST_EARLY, 1))
-            return parts
+        def round_w(group):
+            w_bf[group] = held.tile([P, len(group) * CHUNK_E * N, PACK], BF16, name="w_bf", align_bytes=64)
+            for i, s in enumerate(group):
+                for e in range(CHUNK_E):
+                    col = (i * CHUNK_E + e) * N
+                    nc.gpsimd.tensor_scalar(
+                        w_bf[group][:, col : col + N, :].rearrange("p (c i) t -> p c t i", i=PAIR),
+                        w_raw[s][:, e, :].rearrange("p (t c i) -> p c t i", t=PACK, i=PAIR),
+                        1.0,
+                        0.0,
+                        MULT,
+                        ADD,
+                    )
 
-        def round_w(s):
-            parts = w_parts(s)
-            w_bf[s] = held.tile([P, sum(n for panel, e, n in parts) * N, PACK], BF16, name="w_bf", align_bytes=64)
-            for i, (panel, e, n) in enumerate(parts):
-                nc.gpsimd.tensor_scalar(
-                    w_bf[s][:, i * CHUNK_E * N : (i * CHUNK_E + n) * N, :].rearrange("p (e n) t -> p e n t", n=N),
-                    w_raw[panel][:, e : e + n, :].rearrange("p e (t n) -> p e n t", t=PACK),
-                    1.0,
-                    0.0,
-                    MULT,
-                    ADD,
-                )
-
-        def quantize_w(s):
-            for i, (panel, e, n) in enumerate(w_parts(s)):
-                if e == 0:
-                    pool, tag = (held, "_last") if panel == last_panel else (three, "")
-                    w_codes[panel] = pool.tile([P, CHUNK_E * N], U32, name="w_codes" + tag, align_bytes=64)
-                    w_scales[panel] = pool.tile([P, CHUNK_E * N], U8, name="w_scales" + tag, align_bytes=64)
-                nc.vector.quantize_mx(
-                    out=w_codes[panel][:, e * N : (e + n) * N].bitcast(FP8X4),
-                    scales=w_scales[panel][:, e * N : (e + n) * N],
-                    in_=w_bf[s][:, i * CHUNK_E * N : (i * CHUNK_E + n) * N, :].rearrange("p n t -> p (n t)"),
-                )
+        def quantize_w(group):
+            width = len(group) * CHUNK_E * N
+            pool, tag = (held, "_head") if len(group) > 1 else (three, "")
+            codes = pool.tile([P, width], U32, name="w_codes" + tag, align_bytes=64)
+            scales = pool.tile([P, width], U8, name="w_scales" + tag, align_bytes=64)
+            nc.vector.quantize_mx(
+                out=codes[:].bitcast(FP8X4), scales=scales[:], in_=w_bf[group][:].rearrange("p n t -> p (n t)")
+            )
+            for i, s in enumerate(group):
+                cols = slice(i * CHUNK_E * N, (i + 1) * CHUNK_E * N)
+                w_codes[panels[s]], w_scales[panels[s]] = codes[:, cols], scales[:, cols]
 
         def spread_gate(block):
             gate_rows[block] = psum.tile([P, RUN, P], F32, name="bank%d" % (block % GATE_BANKS))
@@ -163,25 +169,26 @@ def tile_moe_pre_lin_relu2_kernel(
             return tokens[g][t][:].indirect(slot_tokens[:, (first + lo) // STRIPE : (first + hi) // STRIPE])
 
         def vector_share(s, t):
+            width = steps[s][2]
             if s == 0:
-                return CHUNK // 2
-            if t == 0 and s <= FULL_STEPS:
-                return VECTOR_SHARE if s < FULL_STEPS else CLOSING_SHARE
-            return 0
+                return width // 2
+            return min(max(shares.get(s, 0) - t * width, 0), width)
 
         def gather_on_scalar(s, t):
             share, width = vector_share(s, t), steps[s][2]
-            nc.scalar.activation(x_f32[s][:, t, share:width], window(s, t, share, width), COPY)
+            if share < width:
+                nc.scalar.activation(x_f32[s][:, t, share:width], window(s, t, share, width), COPY)
 
         def gather_on_vector(s, t):
             share = vector_share(s, t)
-            nc.vector.tensor_copy(x_f32[s][:, t, 0:share], window(s, t, 0, share))
+            if share:
+                nc.vector.tensor_copy(x_f32[s][:, t, 0:share], window(s, t, 0, share))
 
         def open_step(s):
             x_f32[s] = held.tile([P, PACK, steps[s][2]], F32, name="x_f32_%d" % (s % X_BUFFERS), align_bytes=64)
             for t in range(PACK):
                 gather_on_scalar(s, t)
-                if s == 0:
+                if s < 2:
                     gather_on_vector(s, t)
 
         def times_gate(engine, s, lo, hi, rows):
@@ -194,11 +201,12 @@ def tile_moe_pre_lin_relu2_kernel(
 
         def gate_and_round(s):
             g, first, width = steps[s]
-            tag = "x_bf" if s <= FULL_STEPS else "x_bf%d" % s
-            x_bf[s] = held.tile([P, width, PACK], BF16, name=tag, align_bytes=64)
+            if s <= FULL_STEPS:
+                x_bf["chunk"] = held.tile([P, CHUNK, PACK], BF16, name="x_bf", align_bytes=64)
+            x_bf[s] = x_bf["chunk"][:, first % CHUNK : first % CHUNK + width, :]
             m = pooled.get(s, 0)
             if m:
-                rows = gate_closing[:] if s == FULL_STEPS else gate_early[:, first // CHUNK, :]
+                rows = gate_pool[first // CHUNK][:, 0:m]
                 times_gate(nc.gpsimd, s, 0, m, rows.rearrange("p (c i) -> p c i", i=RUN))
             for start in range(0, width, BANK):
                 lo, hi = max(start, m), min(start + BANK, width)
@@ -211,7 +219,7 @@ def tile_moe_pre_lin_relu2_kernel(
             x_codes[s] = two.tile([P, width], U32, name="x_codes", align_bytes=64)
             x_scales[s] = two.tile([P, width], U8, name="x_scales", align_bytes=64)
             nc.vector.quantize_mx(
-                out=x_codes[s][:].bitcast(FP8X4), scales=x_scales[s][:], in_=x_bf[s][:].rearrange("p c t -> p (c t)")
+                out=x_codes[s][:].bitcast(FP8X4), scales=x_scales[s][:], in_=x_bf[s].rearrange("p c t -> p (c t)")
             )
 
         def multiply(s):
@@ -265,18 +273,18 @@ def tile_moe_pre_lin_relu2_kernel(
         for t in range(2, PACK):
             load_tokens(0, t)
         load_gate_cols(1)
-        nc.sync.dma_start(out=gate_early[:], in_=gate[0:P, :].rearrange("p (c j) -> p c j", c=CHUNKS)[:, 0:2, 0:POOL_SHARE])
-        load_w(panels[0])
+        load_w(0)
+        load_gate_pool(0)
+        load_w(1)
         for t in range(PACK):
             load_tokens(1, t)
-        load_w(panels[1])
-        load_w(panels[2])
+        load_w(2)
+        load_gate_pool(1)
         for t in range(PACK):
             load_tokens(2, t)
         for c in range(2, CHUNKS):
             load_gate_cols(c)
-        nc.sync.dma_start(out=gate_closing[:], in_=gate[0:P, SLOTS - CHUNK : SLOTS - CHUNK + CLOSING_POOL_SHARE])
-        load_w(last_panel)
+            load_gate_pool(c)
         nc.sync.dma_start(out=bias[:], in_=b)
         for r, pos in enumerate((pos1, pos2, pos3, pos4)):
             nc.sync.dma_start(token_slots[r][:], pos)
@@ -285,28 +293,31 @@ def tile_moe_pre_lin_relu2_kernel(
         for block in range(GATE_BANKS):
             spread_gate(block)
 
-        round_w(0)
+        round_w((0, 1))
+        load_w(3)
         open_step(0)
+        open_step(1)
         for s in range(FULL_STEPS):
             g, first, width = steps[s]
-            open_step(s + 1)
-            gather_on_vector(s + 1, 0)
+            open_step(s + 2)
             gate_and_round(s)
             if g == PASSES - 1 and first < 2 * CHUNK:
                 for block in range(first // BANK, (first + width) // BANK):
                     spread_gate(block + GATE_BANKS)
-            quantize_w(s)
-            if s + 1 < FULL_STEPS:
-                round_w(s + 1)
+            for t in range(PACK):
+                gather_on_vector(s + 2, t)
+            quantize_w((0, 1) if s == 0 else (s + 1,))
+            if s + 2 <= FULL_STEPS:
+                round_w((s + 2,))
+            if s + 4 <= FULL_STEPS:
+                load_w(s + 4)
             quantize_x(s)
-            if s + 3 < FULL_STEPS:
-                load_w(panels[s + 3])
             multiply(s)
             activate_finished()
 
         for s in range(FULL_STEPS, last + 1):
-            if s < last:
-                open_step(s + 1)
+            if s + 2 <= last:
+                open_step(s + 2)
             gate_and_round(s)
             for ready in ([s - 1] if s > FULL_STEPS else []) + ([s] if s == last else []):
                 quantize_x(ready)

@@ -40,13 +40,9 @@ X_BUFFERS = 3
 CLOSING_WIDTHS = (512, 256, 128, 128)
 LAST = (E - 1) * C
 PAIR = 2
-VECTOR_SHARE = CHUNK
-HEAD_SHARE = 1536
-CLOSING_SHARE = 512
-POOL_SHARE = 208
-HEAD_POOL_SHARE = 288
-LATE_POOL_SHARE = 128
-CLOSING_POOL_SHARE = 160
+VECTOR_SHARE = 960
+CLOSING_SHARE = 320
+POOL_SHARE = 112
 TOKEN_CUTS = (0, 256, 512, 768, 896, 1024)
 LISTS_ON_SCALAR = (1, 2, 3, 3, 2)
 
@@ -79,14 +75,8 @@ def tile_moe_pre_lin_relu2_kernel(
     last = len(steps) - 1
     panels = [(first // CHUNK, g) for g, first, width in steps]
     pooled = {s: POOL_SHARE for s in range(FULL_STEPS)}
-    pooled[0] = HEAD_POOL_SHARE
-    pooled[FULL_STEPS - 2] = LATE_POOL_SHARE
-    pooled[FULL_STEPS - 1] = LATE_POOL_SHARE
-    pooled[FULL_STEPS] = CLOSING_POOL_SHARE
     shares = {s: VECTOR_SHARE for s in range(FULL_STEPS)}
-    shares[1] = HEAD_SHARE
     shares[FULL_STEPS] = CLOSING_SHARE
-    shares[FULL_STEPS + 1] = CLOSING_SHARE
     pooled_of_chunk = [max(m for s, m in pooled.items() if panels[s][0] == c) for c in range(CHUNKS)]
 
     with ExitStack() as ctx:
@@ -203,7 +193,12 @@ def tile_moe_pre_lin_relu2_kernel(
             g, first, width = steps[s]
             if s <= FULL_STEPS:
                 x_bf["chunk"] = held.tile([P, CHUNK, PACK], BF16, name="x_bf", align_bytes=64)
-            x_bf[s] = x_bf["chunk"][:, first % CHUNK : first % CHUNK + width, :]
+            if first == LAST:
+                x_bf["last"] = held.tile([P, C, PACK], BF16, name="w_bf", align_bytes=64)
+            if first < LAST:
+                x_bf[s] = x_bf["chunk"][:, first % CHUNK : first % CHUNK + width, :]
+            else:
+                x_bf[s] = x_bf["last"][:, first - LAST : first - LAST + width, :]
             m = pooled.get(s, 0)
             if m:
                 rows = gate_pool[first // CHUNK][:, 0:m]
@@ -275,11 +270,11 @@ def tile_moe_pre_lin_relu2_kernel(
         load_gate_cols(1)
         load_w(0)
         load_gate_pool(0)
-        load_w(1)
         for t in range(PACK):
             load_tokens(1, t)
-        load_w(2)
+        load_w(1)
         load_gate_pool(1)
+        load_w(2)
         for t in range(PACK):
             load_tokens(2, t)
         for c in range(2, CHUNKS):
@@ -293,8 +288,7 @@ def tile_moe_pre_lin_relu2_kernel(
         for block in range(GATE_BANKS):
             spread_gate(block)
 
-        round_w((0, 1))
-        load_w(3)
+        round_w((0,))
         open_step(0)
         open_step(1)
         for s in range(FULL_STEPS):
@@ -306,11 +300,10 @@ def tile_moe_pre_lin_relu2_kernel(
                     spread_gate(block + GATE_BANKS)
             for t in range(PACK):
                 gather_on_vector(s + 2, t)
-            quantize_w((0, 1) if s == 0 else (s + 1,))
-            if s + 2 <= FULL_STEPS:
-                round_w((s + 2,))
-            if s + 4 <= FULL_STEPS:
-                load_w(s + 4)
+            quantize_w((s,))
+            round_w((s + 1,))
+            if s + 3 <= FULL_STEPS:
+                load_w(s + 3)
             quantize_x(s)
             multiply(s)
             activate_finished()
@@ -319,6 +312,8 @@ def tile_moe_pre_lin_relu2_kernel(
             if s + 2 <= last:
                 open_step(s + 2)
             gate_and_round(s)
+            if s == FULL_STEPS + 1:
+                quantize_w((FULL_STEPS,))
             for ready in ([s - 1] if s > FULL_STEPS else []) + ([s] if s == last else []):
                 quantize_x(ready)
                 multiply(ready)

@@ -40,9 +40,9 @@ X_BUFFERS = 3
 CLOSING_WIDTHS = (512, 256, 128, 128)
 LAST = (E - 1) * C
 PAIR = 2
-VECTOR_SHARE = 960
+VECTOR_SHARE = 928
 CLOSING_SHARE = 320
-POOL_SHARE = 112
+POOL_SHARE = 128
 TOKEN_CUTS = (0, 256, 512, 768, 896, 1024)
 LISTS_ON_SCALAR = (1, 2, 3, 3, 2)
 

from contextlib import ExitStack

import concourse.mybir as mybir
from concourse.masks import make_identity

K, T, E, C, N = 1536, 1024, 16, 256, 128
TOP = 4
SLOTS = E * C

FLOPS = 2 * K * N * SLOTS
BYTES = 4 * (K * T + E * K * N + N * E + SLOTS + N * T) + 2 * 128 * (SLOTS + TOP * T) // 16

F32 = mybir.dt.float32
BF16 = mybir.dt.bfloat16
U32 = mybir.dt.uint32
U16 = mybir.dt.uint16
U8 = mybir.dt.uint8
FP8X4 = mybir.dt.float8_e4m3fn_x4
MULT = mybir.AluOpType.mult
ADD = mybir.AluOpType.add
MAX = mybir.AluOpType.max
COPY = mybir.ActivationFunctionType.Copy
RELU = mybir.ActivationFunctionType.Relu
SQUARE = mybir.ActivationFunctionType.Square

P = 128
PACK = 4
K_PASS = P * PACK
PASSES = K // K_PASS
STRIPE = 16
CHUNK_E = 4
CHUNK = CHUNK_E * C
CHUNKS = E // CHUNK_E
FULL_STEPS = CHUNKS * PASSES - 1
BANK = 512
GATE_BANKS = 4
SPARE = 16
RUN = 4
X_BUFFERS = 3
CLOSING_WIDTHS = (512, 256, 128, 128)
LAST = (E - 1) * C
PAIR = 2
VECTOR_SHARE = 928
CLOSING_SHARE = 320
POOL_SHARE = 128
TOKEN_CUTS = (0, 256, 512, 768, 896, 1024)
LISTS_ON_SCALAR = (1, 2, 3, 3, 2)


def make_steps():
    steps = [(g, chunk * CHUNK, CHUNK) for g in range(PASSES) for chunk in range(2)]
    steps = steps + [(g, chunk * CHUNK, CHUNK) for chunk in range(2, CHUNKS) for g in range(PASSES)][:-1]
    first = SLOTS - CHUNK
    for width in CLOSING_WIDTHS:
        steps.append((PASSES - 1, first, width))
        first = first + width
    return steps


def sum_of(slot):
    if slot >= LAST:
        half = (slot - LAST) // (C // 2)
        return LAST + half * (C // 2), C // 2, half
    bank = GATE_BANKS + (slot // BANK) % GATE_BANKS
    if slot >= LAST - C:
        return LAST - C, C, bank
    return slot - slot % BANK, BANK, bank


def tile_moe_pre_lin_relu2_kernel(
    tc, xT, w, b, gate, offs, pos1, pos2, pos3, pos4, out
):
    nc = tc.nc
    steps = make_steps()
    last = len(steps) - 1
    panels = [(first // CHUNK, g) for g, first, width in steps]
    pooled = {s: POOL_SHARE for s in range(FULL_STEPS)}
    shares = {s: VECTOR_SHARE for s in range(FULL_STEPS)}
    shares[FULL_STEPS] = CLOSING_SHARE
    pooled_of_chunk = [max(m for s, m in pooled.items() if panels[s][0] == c) for c in range(CHUNKS)]

    with ExitStack() as ctx:
        held = ctx.enter_context(tc.tile_pool(name="held", bufs=1))
        three = ctx.enter_context(tc.tile_pool(name="three", bufs=3))
        two = ctx.enter_context(tc.tile_pool(name="two", bufs=2))
        psum = ctx.enter_context(tc.psum_pool(name="psum", bufs=1))

        slot_tokens = held.tile([P, SLOTS // STRIPE], U16, name="slot_tokens")
        token_slots = [held.tile([P, T // STRIPE], U16, name="token_slots%d" % r) for r in range(TOP)]
        bias = held.tile([P, E], F32, name="bias")
        identity = held.tile([P, P], F32, name="identity")
        gate_cols = [
            held.tile([P, CHUNK // BANK, RUN], F32, name="x_f32_1" if c == 1 else "gate_cols%d" % c, align_bytes=64)
            for c in range(CHUNKS)
        ]
        gate_pool = [held.tile([P, pooled_of_chunk[c]], F32, name="gate_pool%d" % c) for c in range(CHUNKS)]
        y = held.tile([P, SLOTS], F32, name="y")
        tokens = [
            [held.tile([P, T + SPARE], F32, name="tokens%d_%d" % (g, t), align_bytes=64) for t in range(PACK)]
            for g in range(PASSES)
        ]
        x_rows = xT.rearrange("(g p t) c -> g t p c", g=PASSES, t=PACK)

        w_raw, w_bf, w_codes, w_scales = {}, {}, {}, {}
        x_f32, x_bf, x_codes, x_scales = {}, {}, {}, {}
        gate_rows, sums, done = {}, {}, {}

        def load_tokens(g, t):
            nc.sync.dma_start(out=tokens[g][t][:, 0:T], in_=x_rows[g, t])

        def load_gate_cols(c):
            row = gate[0, c * CHUNK : (c + 1) * CHUNK]
            nc.sync.dma_start(out=gate_cols[c][:], in_=row.rearrange("(h p i) -> p h i", p=P, i=RUN))

        def load_gate_pool(c):
            nc.sync.dma_start(out=gate_pool[c][:], in_=gate[0:P, c * CHUNK : c * CHUNK + pooled_of_chunk[c]])

        def load_w(s):
            chunk, g = panels[s]
            w_raw[s] = three.tile([P, CHUNK_E, PACK * N], F32, name="w_raw", align_bytes=64)
            rows = w[chunk * CHUNK_E : (chunk + 1) * CHUNK_E, g * K_PASS : (g + 1) * K_PASS, :]
            nc.sync.dma_start(out=w_raw[s][:], in_=rows.rearrange("e (p t) n -> p e (t n)", t=PACK))

        def round_w(group):
            w_bf[group] = held.tile([P, len(group) * CHUNK_E * N, PACK], BF16, name="w_bf", align_bytes=64)
            for i, s in enumerate(group):
                for e in range(CHUNK_E):
                    col = (i * CHUNK_E + e) * N
                    nc.gpsimd.tensor_scalar(
                        w_bf[group][:, col : col + N, :].rearrange("p (c i) t -> p c t i", i=PAIR),
                        w_raw[s][:, e, :].rearrange("p (t c i) -> p c t i", t=PACK, i=PAIR),
                        1.0,
                        0.0,
                        MULT,
                        ADD,
                    )

        def quantize_w(group):
            width = len(group) * CHUNK_E * N
            pool, tag = (held, "_head") if len(group) > 1 else (three, "")
            codes = pool.tile([P, width], U32, name="w_codes" + tag, align_bytes=64)
            scales = pool.tile([P, width], U8, name="w_scales" + tag, align_bytes=64)
            nc.vector.quantize_mx(
                out=codes[:].bitcast(FP8X4), scales=scales[:], in_=w_bf[group][:].rearrange("p n t -> p (n t)")
            )
            for i, s in enumerate(group):
                cols = slice(i * CHUNK_E * N, (i + 1) * CHUNK_E * N)
                w_codes[panels[s]], w_scales[panels[s]] = codes[:, cols], scales[:, cols]

        def spread_gate(block):
            gate_rows[block] = psum.tile([P, RUN, P], F32, name="bank%d" % (block % GATE_BANKS))
            chunk, h = divmod(block, CHUNK // BANK)
            for i in range(RUN):
                column = gate_cols[chunk][:, h, i : i + 1].to_broadcast([P, P])
                nc.tensor.transpose(gate_rows[block][:, i, :], column, identity[:])

        def window(s, t, lo, hi):
            g, first, width = steps[s]
            return tokens[g][t][:].indirect(slot_tokens[:, (first + lo) // STRIPE : (first + hi) // STRIPE])

        def vector_share(s, t):
            width = steps[s][2]
            if s == 0:
                return width // 2
            return min(max(shares.get(s, 0) - t * width, 0), width)

        def gather_on_scalar(s, t):
            share, width = vector_share(s, t), steps[s][2]
            if share < width:
                nc.scalar.activation(x_f32[s][:, t, share:width], window(s, t, share, width), COPY)

        def gather_on_vector(s, t):
            share = vector_share(s, t)
            if share:
                nc.vector.tensor_copy(x_f32[s][:, t, 0:share], window(s, t, 0, share))

        def open_step(s):
            x_f32[s] = held.tile([P, PACK, steps[s][2]], F32, name="x_f32_%d" % (s % X_BUFFERS), align_bytes=64)
            for t in range(PACK):
                gather_on_scalar(s, t)
                if s < 2:
                    gather_on_vector(s, t)

        def times_gate(engine, s, lo, hi, rows):
            engine.tensor_tensor(
                x_bf[s][:, lo:hi, :].rearrange("p (c i) t -> p c t i", i=RUN),
                x_f32[s][:, :, lo:hi].rearrange("p t (c i) -> p c t i", i=RUN),
                rows.unsqueeze(2).to_broadcast([P, (hi - lo) // RUN, PACK, RUN]),
                MULT,
            )

        def gate_and_round(s):
            g, first, width = steps[s]
            if s <= FULL_STEPS:
                x_bf["chunk"] = held.tile([P, CHUNK, PACK], BF16, name="x_bf", align_bytes=64)
            if first == LAST:
                x_bf["last"] = held.tile([P, C, PACK], BF16, name="w_bf", align_bytes=64)
            if first < LAST:
                x_bf[s] = x_bf["chunk"][:, first % CHUNK : first % CHUNK + width, :]
            else:
                x_bf[s] = x_bf["last"][:, first - LAST : first - LAST + width, :]
            m = pooled.get(s, 0)
            if m:
                rows = gate_pool[first // CHUNK][:, 0:m]
                times_gate(nc.gpsimd, s, 0, m, rows.rearrange("p (c i) -> p c i", i=RUN))
            for start in range(0, width, BANK):
                lo, hi = max(start, m), min(start + BANK, width)
                block, col = divmod(first + lo, BANK)
                rows = gate_rows[block][:, :, col // RUN : (col + hi - lo) // RUN]
                times_gate(nc.vector, s, lo, hi, rows.rearrange("p i c -> p c i"))

        def quantize_x(s):
            width = steps[s][2]
            x_codes[s] = two.tile([P, width], U32, name="x_codes", align_bytes=64)
            x_scales[s] = two.tile([P, width], U8, name="x_scales", align_bytes=64)
            nc.vector.quantize_mx(
                out=x_codes[s][:].bitcast(FP8X4), scales=x_scales[s][:], in_=x_bf[s].rearrange("p c t -> p (c t)")
            )

        def multiply(s):
            g, first, width = steps[s]
            lo = first
            while lo < first + width:
                base, group, bank = sum_of(lo)
                size = min(group, C)
                if base not in done:
                    sums[base] = psum.tile([P, group], F32, name="bank%d" % bank)
                    done[base] = 0
                e = (lo // C) % CHUNK_E
                w_cols = slice(e * N, (e + 1) * N)
                x_cols = slice(lo - first, lo - first + size)
                nc.tensor.matmul_mx(
                    out=sums[base][:, lo - base : lo - base + size],
                    lhsT=w_codes[panels[s]][:, w_cols].bitcast(FP8X4),
                    lhsT_scale=w_scales[panels[s]][:, w_cols],
                    rhs=x_codes[s][:, x_cols].bitcast(FP8X4),
                    rhs_scale=x_scales[s][:, x_cols],
                    start=(done[base] == 0),
                    stop=(done[base] + size == PASSES * group),
                )
                done[base] = done[base] + size
                lo = lo + size

        def activate_finished():
            for base in sorted(sums):
                group = sum_of(base)[1]
                if done[base] == PASSES * group and base < LAST:
                    bank = sums.pop(base)
                    size = min(group, C)
                    for lo in range(0, group, size):
                        expert = (base + lo) // C
                        nc.scalar.activation(
                            y[:, base + lo : base + lo + size],
                            bank[:, lo : lo + size],
                            RELU,
                            bias=bias[:, expert : expert + 1],
                        )
                    nc.scalar.activation(y[:, base : base + group], y[:, base : base + group], SQUARE)

        unread = held.tile([P, 2], F32, name="unread")
        nc.vector.memset(unread[:, 0:1], 0.0)
        nc.scalar.activation(unread[:, 1:2], unread[:, 0:1], RELU)

        load_tokens(0, 0)
        nc.sync.dma_start(slot_tokens[:], offs)
        load_tokens(0, 1)
        load_gate_cols(0)
        for t in range(2, PACK):
            load_tokens(0, t)
        load_gate_cols(1)
        load_w(0)
        load_gate_pool(0)
        for t in range(PACK):
            load_tokens(1, t)
        load_w(1)
        load_gate_pool(1)
        load_w(2)
        for t in range(PACK):
            load_tokens(2, t)
        for c in range(2, CHUNKS):
            load_gate_cols(c)
            load_gate_pool(c)
        nc.sync.dma_start(out=bias[:], in_=b)
        for r, pos in enumerate((pos1, pos2, pos3, pos4)):
            nc.sync.dma_start(token_slots[r][:], pos)

        make_identity(nc, identity[:])
        for block in range(GATE_BANKS):
            spread_gate(block)

        round_w((0,))
        open_step(0)
        open_step(1)
        for s in range(FULL_STEPS):
            g, first, width = steps[s]
            open_step(s + 2)
            gate_and_round(s)
            if g == PASSES - 1 and first < 2 * CHUNK:
                for block in range(first // BANK, (first + width) // BANK):
                    spread_gate(block + GATE_BANKS)
            for t in range(PACK):
                gather_on_vector(s + 2, t)
            quantize_w((s,))
            round_w((s + 1,))
            if s + 3 <= FULL_STEPS:
                load_w(s + 3)
            quantize_x(s)
            multiply(s)
            activate_finished()

        for s in range(FULL_STEPS, last + 1):
            if s + 2 <= last:
                open_step(s + 2)
            gate_and_round(s)
            if s == FULL_STEPS + 1:
                quantize_w((FULL_STEPS,))
            for ready in ([s - 1] if s > FULL_STEPS else []) + ([s] if s == last else []):
                quantize_x(ready)
                multiply(ready)
                activate_finished()

        halves = [(base, y[:, base : base + C // 2]) for base in sorted(sums)]
        for base, half in halves:
            nc.vector.tensor_scalar(half, sums[base][:], bias[:, E - 1 : E], 0.0, ADD, MAX)
        for base, half in halves:
            nc.vector.tensor_tensor(half, half, half, MULT)

        picked = held.tile([P, TOP - 1, T], F32, name="picked")
        pairs = held.tile([P, 2, T], F32, name="pairs")
        total = held.tile([P, T], F32, name="total")
        blocks = [slice(lo, hi) for lo, hi in zip(TOKEN_CUTS[:-1], TOKEN_CUTS[1:])]
        final = len(blocks) - 1

        def results(r, cols):
            return y[:].indirect(token_slots[r][:, cols.start // STRIPE : cols.stop // STRIPE])

        def finish(i, queue):
            cols = blocks[i]
            nc.vector.tensor_tensor(total[:, cols], pairs[:, 0, cols], pairs[:, 1, cols], ADD)
            queue.dma_start(out=out[:, cols], in_=total[:, cols])

        for i, cols in enumerate(blocks):
            on_scalar = LISTS_ON_SCALAR[i]
            for r in range(on_scalar):
                nc.scalar.activation(picked[:, r, cols], results(r, cols), COPY)
            if on_scalar == 1:
                nc.vector.tensor_copy(picked[:, 1, cols], results(1, cols))
            nc.vector.tensor_tensor(pairs[:, 0, cols], results(3, cols), picked[:, 0, cols], ADD)
            if 0 < i < final:
                finish(i - 1, nc.sync)
            third = picked[:, 2, cols] if on_scalar == 3 else results(2, cols)
            nc.vector.tensor_tensor(pairs[:, 1, cols], third, picked[:, 1, cols], ADD)
        finish(final - 1, nc.scalar)
        finish(final, nc.sync)
